import numpy as np
import ml_dtypes


def mxq(x, axis, fmt="e4m3"):
    dtype, down = {"e4m3": (ml_dtypes.float8_e4m3fn, 7), "e5m2": (ml_dtypes.float8_e5m2, 14)}[fmt]
    v = np.moveaxis(np.asarray(x, np.float32).astype(ml_dtypes.bfloat16).astype(np.float64), axis, -1)
    blocks = v.reshape(v.shape[:-1] + (-1, 32))
    amax = np.abs(blocks).max(-1, keepdims=True)
    byte = np.maximum(np.where(amax > 0, np.frexp(amax)[1] - 1 + 127, 0) - down, 1)
    scale = np.exp2(byte - 127.0)
    codes = (blocks / scale).astype(np.float32).astype(dtype).astype(np.float64)
    return np.moveaxis((codes * scale).reshape(v.shape), -1, axis)


WIDE = False


def mx_kscale(k):
    if not WIDE:
        return np.ones(k)
    levels = np.array([10, -10, 5, -5, 0])
    if k % 512:
        return np.exp2(np.random.permutation(np.resize(levels, k // 32))).repeat(32)
    a = np.empty((k // 512, 16))
    for p in range(k // 512):
        a[p, :8] = np.random.permutation(np.resize(levels, 8))
        for g in range(8):
            far = levels[np.abs(levels - a[p, g]) >= 10]
            a[p, g + 8] = far[np.random.randint(len(far))]
    return np.exp2(a.ravel()).repeat(32)


def f64(x):
    return np.asarray(x).astype(np.float64)


def striped(idx):
    return np.tile(idx.reshape(-1, 16).T, (8, 1)).astype(np.uint16)


def unstriped(offs):
    return offs[:16].T.reshape(-1).astype(np.int64)


E2M1 = np.array([0.0, 0.5, 1.0, 1.5, 2.0, 3.0, 4.0, 6.0, -0.0, -0.5, -1.0, -1.5, -2.0, -3.0, -4.0, -6.0])


def pack_weight(w, fmt):
    k, n = w.shape
    w = f64(np.asarray(w, np.float32).astype(ml_dtypes.bfloat16)).reshape(k // 32, 32, n)
    amax = np.abs(w).max(1)
    if fmt == "e4m3":
        byte = np.frexp(amax)[1] - 1 + 127 - 7
    else:
        mant, ex = np.frexp(amax / 6.0)
        byte = np.where(mant > 0.5, ex, ex - 1) + 127
    byte = np.clip(np.where(amax > 0, byte, 1), 1, 254)
    scaled = (w * np.exp2(127.0 - byte)[:, None, :]).reshape(k, n).astype(np.float32)
    by_word = np.ascontiguousarray(scaled.reshape(k // 512, 128, 4, n).transpose(0, 1, 3, 2))
    if fmt == "e4m3":
        words = by_word.astype(ml_dtypes.float8_e4m3fn).view(np.uint8)
    else:
        c = by_word.astype(ml_dtypes.float4_e2m1fn).view(np.uint8) & 0xF
        words = (c[..., 0::2] | (c[..., 1::2] << 4)).reshape(k // 512, 128, 2 * n)
    return np.ascontiguousarray(words), np.ascontiguousarray(byte.astype(np.uint8).reshape(k // 512, 16, n))


def unpack_weight(words, scales, fmt):
    g, _, n = scales.shape
    words = np.ascontiguousarray(words).reshape(g, 128, n, -1)
    if fmt == "e4m3":
        vals = words.view(ml_dtypes.float8_e4m3fn).astype(np.float64)
    else:
        nib = np.empty((g, 128, n, 4), np.uint8)
        nib[..., 0::2] = words & 0xF
        nib[..., 1::2] = words >> 4
        vals = E2M1[nib]
    vals = vals * np.repeat(np.exp2(scales.astype(np.float64) - 127.0), 8, axis=1)[..., None]
    return vals.transpose(0, 1, 3, 2).reshape(g * 512, n)


def gelu(v):
    return 0.5 * v * (1.0 + np.tanh(np.sqrt(2.0 / np.pi) * (v + 0.044715 * v**3)))


def striped8(idx):
    return np.concatenate([v.reshape(-1, 16).T for v in idx]).astype(np.uint16)


def unstriped8(offs):
    return np.stack([offs[16 * g:16 * g + 16].T.reshape(-1) for g in range(8)]).astype(np.int64)


def heads(h, wgt, idx8):
    r = np.arange(h.shape[0])
    return wgt[r // 4 % 128] * h[r[:, None], idx8[r % 512 // 64]]


def put_heads(h, wgs, idx8, t2):
    r = np.arange(h.shape[0])
    page = np.zeros((h.shape[0], t2))
    page[r[:, None], idx8[r % 512 // 64]] = wgs[r // 4 % 128] * h
    return page


K, T, S, P, T2, H, N = 512, 4096, 1024, 1024, 2048, 1024, 768

def setup_inputs():
    n = np.random.standard_normal
    s = mx_kscale(K)[:, None]
    u = mx_kscale(H)[:, None]
    d = {}
    d["tab_words"], d["tab_scales"] = pack_weight(n((K, T)) * s, "e4m3")
    d["offs"] = striped(np.random.permutation(T)[:S])
    d["w1"] = (n((K, H)) / K**0.5 / s * u.T).astype(np.float32)
    d["b1"] = (0.5 * n(H) * u[:, 0]).astype(np.float32)
    d["w2_words"], d["w2_scales"] = pack_weight(n((K, H)) / K**0.5 / s * u.T, "e2m1")
    d["wgs"] = np.repeat(np.random.uniform(0.5, 2.0, (8, S)), 16, axis=0).astype(np.float32)
    d["offs2"] = striped8(np.stack([np.random.permutation(T2)[:S] for _ in range(8)]))
    d["wgt"] = np.repeat(np.random.uniform(0.5, 2.0, (8, P)), 16, axis=0).astype(np.float32)
    d["offs3"] = striped8(np.stack([np.random.permutation(T2)[:P] for _ in range(8)]))
    d["heat"] = (2.5 * n((H, P))).astype(np.float32)
    d["hg"] = (0.3 * np.exp(0.3 * n(H)) * u[:, 0]).astype(np.float32)
    d["w3"] = (n((H, N)) / H**0.5 / u).astype(np.float32)
    d["w4_words"], d["w4_scales"] = pack_weight(0.8 * n((K, N)) / K**0.5 / s, "e4m3")
    return d

def reference(tab_words, tab_scales, offs, w1, b1, w2_words, w2_scales, wgs, offs2, wgt, offs3, heat, hg, w3, w4_words, w4_scales):
    v = unpack_weight(tab_words, tab_scales, "e4m3")[:, unstriped(offs)]
    W1 = mxq(f64(w1), 0, "e4m3")
    W2 = unpack_weight(w2_words, w2_scales, "e2m1")
    h = np.maximum((W1.T @ v) + f64(b1)[:, None], W2.T @ v)
    page = put_heads(h, f64(wgs), unstriped8(offs2), T2)
    x = heads(page, f64(wgt), unstriped8(offs3))
    ht = f64(heat)
    z = x * (1.0 / (1.0 + np.exp(-ht))) + f64(hg)[:, None] * ht
    W3 = mxq(f64(w3), 0, "e4m3")
    W4 = unpack_weight(w4_words, w4_scales, "e4m3")
    return W3.T @ mxq(z, 0, "e4m3") + W4.T @ v

@@ -1,0 +1,323 @@
+from contextlib import ExitStack
+
+import concourse.mybir as mybir
+from concourse.masks import make_identity
+
+K, T, S, T2, H, N = 512, 4096, 1024, 2048, 1024, 768
+FLOPS = 2 * K * H * S * 2 + 2 * H * N * S + 2 * K * N * S
+
+F32 = mybir.dt.float32
+BF16 = mybir.dt.bfloat16
+I32 = mybir.dt.int32
+U32 = mybir.dt.uint32
+U16 = mybir.dt.uint16
+U8 = mybir.dt.uint8
+FP8X4 = mybir.dt.float8_e4m3fn_x4
+FP4X4 = mybir.dt.float4_e2m1fn_x4
+ALU = mybir.AluOpType
+ACT = mybir.ActivationFunctionType
+
+P = 128
+HALF = 512
+POOL = True
+TAIL = [(256, "pe", [0, 1, 2], "sss"), (256, "v", [3, 7, 4], "sss"), (256, "v", [5, 6, 0], "sss"), (128, "v", [1, 2], "ss"), (128, "v", [3, 7], "sv")]
+
+
+def tile_list_roast_phase_scores_kernel(tc, tab_words, tab_scales, offs, w1, b1, w2_words, w2_scales, wgs, offs2, wgt,
+                                                  offs3, heat, hg, w3, w4_words, w4_scales, out):
+    nc = tc.nc
+    with ExitStack() as ctx:
+        keep = ctx.enter_context(tc.tile_pool(name="keep", bufs=1))
+        ring = ctx.enter_context(tc.tile_pool(name="ring", bufs=2))
+        psum = ctx.enter_context(tc.psum_pool(name="psum", bufs=1))
+
+        def bank(number, name):
+            return psum.tile([P, HALF], F32, tag="bank%d" % number, name=name)
+
+        def load_scale_rows(queue, plane, rows):
+            for quad in range(4):
+                queue.dma_start(out=plane[32 * quad:32 * quad + 4, :].bitcast(I32), in_=rows[4 * quad:4 * quad + 4, :].bitcast(I32))
+
+        list1 = keep.tile([P, S // 16], U16, name="list1")
+        list2 = keep.tile([P, S // 16], U16, name="list2")
+        list3 = keep.tile([P, S // 16], U16, name="list3")
+        tab_s = keep.tile([P, T], U8, name="tab_s", align_bytes=64)
+        w2_s_raw = keep.tile([P, H], U8, name="w2_s_raw", align_bytes=64)
+        w4_s = keep.tile([P, N], U8, name="w4_s", align_bytes=64)
+        nc.vector.memset(w2_s_raw[:].bitcast(I32), 0)
+        nc.vector.memset(tab_s[:].bitcast(I32), 0)
+        nc.vector.memset(w4_s[:].bitcast(I32), 0)
+
+        warm = keep.tile([P, 1], F32, name="warm")
+        nc.vector.memset(warm[:], 0.0)
+        nc.scalar.activation(warm[:], warm[:], ACT.Sigmoid)
+
+        w2_raw = keep.tile([P, 2 * H], U8, name="w2_raw", align_bytes=64)
+        nc.sync.dma_start(out=w2_raw[:].bitcast(I32), in_=w2_words[0].bitcast(I32))
+        tab_w = keep.tile([P, T], I32, name="tab_w", tag="table", align_bytes=64)
+        nc.sync.dma_start(out=tab_w[:], in_=tab_words[0].rearrange("p t i -> p (t i)").bitcast(I32))
+        nc.sync.dma_start(list1[:], offs)
+        load_scale_rows(nc.gpsimd, w2_s_raw, w2_scales[0])
+        load_scale_rows(nc.sync, tab_s, tab_scales[0])
+
+        w1_raw = [keep.tile([P, 4, HALF], F32, name="w1_raw0", tag="gate_0", align_bytes=64),
+                  keep.tile([P, 4, HALF], F32, name="w1_raw1", tag="w3_grouped", align_bytes=64)]
+        nc.sync.dma_start(out=w1_raw[0][:], in_=w1[:, 0:HALF].rearrange("(p t) c -> p t c", t=4))
+        b1_sb = keep.tile([P, 2, 4], F32, name="b1_sb")
+        nc.sync.dma_start(out=b1_sb[:], in_=b1.rearrange("(b p i) -> p b i", b=2, i=4))
+        wgs_sb = keep.tile([P, S], F32, name="wgs_sb")
+        nc.sync.dma_start(out=wgs_sb[:], in_=wgs)
+        nc.sync.dma_start(list2[:], offs2)
+        heat_sb = [keep.tile([P, 4, S], F32, name="heat%d" % b) for b in range(2)]
+        wgt_sb = keep.tile([P, S], F32, name="wgt_sb")
+        nc.sync.dma_start(out=wgt_sb[:], in_=wgt)
+        for u in range(2):
+            nc.sync.dma_start(out=heat_sb[0][:, 2 * u:2 * u + 2, :], in_=heat[0:HALF, :].rearrange("(p i) j -> p i j", i=4)[:, 2 * u:2 * u + 2, :])
+        hg_sb = keep.tile([P, 2, 4], F32, name="hg_sb")
+        nc.sync.dma_start(out=hg_sb[:], in_=hg.rearrange("(b p i) -> p b i", b=2, i=4))
+        nc.sync.dma_start(list3[:], offs3)
+        nc.sync.dma_start(out=w1_raw[1][:], in_=w1[:, HALF:H].rearrange("(p t) c -> p t c", t=4))
+        nc.sync.dma_start(out=heat_sb[1][:], in_=heat[HALF:H, :].rearrange("(p i) j -> p i j", i=4))
+        w4_w = keep.tile([P, N], I32, name="w4_w", align_bytes=64)
+        nc.sync.dma_start(out=w4_w[:], in_=w4_words[0].rearrange("p c i -> p (c i)").bitcast(I32))
+        load_scale_rows(nc.sync, w4_s, w4_scales[0])
+        w3_raw0 = keep.tile([P, 4, N], F32, name="w3_raw0", tag="h_last", align_bytes=64)
+        nc.sync.dma_start(out=w3_raw0[:], in_=w3[0:HALF, :].rearrange("(p i) n -> p i n", i=4))
+
+        ident = keep.tile([P, P], F32, name="ident")
+        make_identity(nc, ident[:])
+
+        pages = [keep.tile([P, T2], F32, name="page%d" % i) for i in range(3)]
+        for page in pages:
+            nc.vector.memset(page[:], 0.0)
+
+        w2_w = keep.tile([P, 2, 4, P, 2], U8, name="w2_w", align_bytes=64)
+        w2_s = keep.tile([P, 2, 4, P], U8, name="w2_s", align_bytes=64)
+        for b in range(2):
+            nc.vector.tensor_copy(out=w2_w[:, b], in_=w2_raw[:, 2 * HALF * b:2 * HALF * (b + 1)].rearrange("p (q i e) -> p i q e", i=4, e=2))
+        nc.vector.tensor_copy(out=w2_s[:], in_=w2_s_raw[:].rearrange("p (b q i) -> p b i q", b=2, i=4))
+
+        v_w = keep.tile([P, S], U32, name="v_w", align_bytes=64)
+        v_s = {}
+
+        def pick_words(half):
+            nc.vector.tensor_copy(v_w[:, HALF * half:HALF * (half + 1)], tab_w[:].bitcast(U32).indirect(list1[:, 32 * half:32 * (half + 1)]))
+
+        def pick_scales(half, tag):
+            v_s[half] = keep.tile([P, HALF], U8, name="v_s%d" % half, tag=tag, align_bytes=64)
+            nc.vector.tensor_copy(v_s[half][:], tab_s[:].indirect(list1[:, 32 * half:32 * (half + 1)]))
+
+        w1_w = keep.tile([P, 8 * P], U32, name="w1_w", align_bytes=64)
+        w1_s = keep.tile([P, 8 * P], U8, name="w1_s", align_bytes=64)
+
+        def quantize_w1(b, u, tag):
+            grouped = keep.tile([P, 2, P, 4], BF16, name="w1_grouped", tag=tag, align_bytes=64)
+            nc.scalar.copy(out=grouped[:].rearrange("p e q t -> p q t e"),
+                           in_=w1_raw[b][:].rearrange("p t (q i) -> p q t i", i=4)[:, :, :, 2 * u:2 * u + 2])
+            cols = slice((4 * b + 2 * u) * P, (4 * b + 2 * u + 2) * P)
+            nc.vector.quantize_mx(out=w1_w[:, cols].bitcast(FP8X4), scales=w1_s[:, cols], in_=grouped[:].rearrange("p e q t -> p (e q t)"))
+
+        w3_s = keep.tile([P, 2 * N], U8, name="w3_s", align_bytes=64)
+
+        def round_w3(raw, b):
+            for third in range(3):
+                cols = slice(256 * third, 256 * (third + 1))
+                nc.scalar.copy(out=w3_grouped[:, N * b + cols.start:N * b + cols.stop, :].rearrange("p (c e) t -> p c t e", e=4),
+                               in_=raw[:, :, cols].rearrange("p t (c e) -> p c t e", e=4))
+
+        h_tiles = {}
+
+        def first_stage(s, h):
+            b, i = divmod(s, 4)
+            wcols = slice(P * s, P * (s + 1))
+            biased = ring.tile([P, S], F32, name="biased", tag="biased")
+            h_tiles[s] = h
+            for half in range(2):
+                cols = slice(HALF * half, HALF * (half + 1))
+                read1 = bank(half, "read1")
+                nc.tensor.matmul_mx(out=read1[:], lhsT=w1_w[:, wcols].bitcast(FP8X4), lhsT_scale=w1_s[:, wcols],
+                                    rhs=v_w[:, cols].bitcast(FP8X4), rhs_scale=v_s[half][:], start=True, stop=True)
+                read2 = bank(2 + half, "read2")
+                nc.tensor.matmul_mx(out=read2[:], lhsT=w2_w[:, b, i].rearrange("p q e -> p (q e)").bitcast(FP4X4), lhsT_scale=w2_s[:, b, i],
+                                    rhs=v_w[:, cols].bitcast(FP8X4), rhs_scale=v_s[half][:], start=True, stop=True)
+                nc.scalar.activation(biased[:, cols], read1[:], ACT.Identity, bias=b1_sb[:, b, i:i + 1])
+                nc.vector.tensor_tensor(h[:, cols], read2[:], biased[:, cols], ALU.max)
+                if POOL:
+                    nc.gpsimd.tensor_tensor(h[:, cols], h[:, cols], wgs_sb[:, cols], ALU.mult)
+
+        def place(s, parts=1):
+            h = h_tiles[s]
+            for part in range(parts):
+                cols = slice(S // parts * part, S // parts * (part + 1))
+                window = pages[s % 4][:].indirect(list2[:, cols.start // 16:cols.stop // 16])
+                if POOL:
+                    nc.vector.tensor_copy(window, h[:, cols])
+                else:
+                    nc.vector.tensor_tensor(window, h[:, cols], wgs_sb[:, cols], ALU.mult)
+
+        def heat_terms(s, gate_halves):
+            b, i = divmod(s, 4)
+            for half in range(2):
+                cols = slice(HALF * half, HALF * (half + 1))
+                gate = gate_halves[half][:, i, :]
+                nc.scalar.activation(gate, heat_sb[b][:, i, cols], ACT.Sigmoid)
+                eng = nc.gpsimd if POOL else nc.vector
+                eng.tensor_tensor(gate, gate, wgt_sb[:, cols], ALU.mult)
+
+        def scale_heat(b):
+            for i in range(4):
+                nc.scalar.activation(heat_sb[b][:, i, :], heat_sb[b][:, i, :], ACT.Copy, scale=hg_sb[:, b, i:i + 1])
+
+        z_w = {1: keep.tile([P, S], U32, name="z_w1", align_bytes=64)}
+        z_s = [keep.tile([P, S], U8, name="z_s%d" % b, align_bytes=64) for b in range(2)]
+
+        def read_pages(x, gate_halves, j0, width, order=(0, 1, 2, 3)):
+            half, g0 = divmod(j0, HALF)
+            for i in order:
+                nc.vector.tensor_tensor(x[:, i, j0:j0 + width], pages[i][:].indirect(list3[:, j0 // 16:(j0 + width) // 16]),
+                                        gate_halves[half][:, i, g0:g0 + width], ALU.mult)
+
+        def finish_z(b, x, j0, width, road):
+            z = ring.tile([P, width, 4], BF16, name="z", tag="z", align_bytes=64)
+            hh = heat_sb[b]
+            cols = slice(j0, j0 + width)
+            if road == "v":
+                nc.vector.tensor_tensor(z[:].rearrange("p (c e) i -> p c i e", e=4), x[:, :, cols].rearrange("p i (c e) -> p c i e", e=4),
+                                        hh[:, :, cols].rearrange("p i (c e) -> p c i e", e=4), ALU.add)
+            else:
+                z_words = z[:].rearrange("p j i -> p (j i)").bitcast(F32).rearrange("p (j u) -> p j u", u=2)
+                for pair in range(width // 256):
+                    back = bank(6, "back")
+                    for blk in range(2):
+                        c0 = j0 + 256 * pair + P * blk
+                        turned = bank(4 + blk, "turned")
+                        for i in range(4):
+                            nc.tensor.matmul(turned[:, P * i:P * (i + 1)], lhsT=hh[:, i, c0:c0 + P], rhs=ident[:],
+                                             is_transpose=True, start=(i == 0), stop=False)
+                        for i in range(4):
+                            nc.tensor.matmul(turned[:, P * i:P * (i + 1)], lhsT=x[:, i, c0:c0 + P], rhs=ident[:],
+                                             is_transpose=True, start=False, stop=(i == 3))
+                        z_turned = ring.tile([P, 2, P, 2], BF16, name="z_turned", tag="z_turned")
+                        nc.scalar.copy(out=z_turned[:], in_=turned[:].rearrange("j (u e p) -> j u p e", u=2, e=2))
+                        words = z_turned[:].rearrange("j u p e -> j (u p e)").bitcast(F32)
+                        for u in range(2):
+                            nc.tensor.transpose(back[:, 256 * blk + P * u:256 * blk + P * (u + 1)], words[:, P * u:P * (u + 1)], ident[:])
+                    nc.scalar.copy(out=z_words[:, 256 * pair:256 * (pair + 1), :].rearrange("p (k j) u -> p k j u", k=2),
+                                   in_=back[:].rearrange("p (k u j) -> p k j u", k=2, u=2))
+            return z
+
+        def quantize_z(b, z, j0, width):
+            cols = slice(j0, j0 + width)
+            nc.vector.quantize_mx(out=z_w[b][:, cols].bitcast(FP8X4), scales=z_s[b][:, cols], in_=z[:].rearrange("p j i -> p (j i)"))
+
+        def open_scores(number, tiles, j0, width):
+            acc = bank(number, "acc")
+            cols = slice(j0, j0 + width)
+            half, g0 = divmod(j0, HALF)
+            for k, n in enumerate(tiles):
+                ncols = slice(P * n, P * (n + 1))
+                nc.tensor.matmul_mx(out=acc[:, width * k:width * (k + 1)], lhsT=w4_w[:, ncols].bitcast(FP8X4), lhsT_scale=w4_s[:, ncols],
+                                    rhs=v_w[:, cols].bitcast(FP8X4), rhs_scale=v_s[half][:, g0:g0 + width], start=(k == 0), stop=False)
+                nc.tensor.matmul_mx(out=acc[:, width * k:width * (k + 1)], lhsT=w3_w[:, ncols].bitcast(FP8X4), lhsT_scale=w3_s[:, ncols],
+                                    rhs=z_w[0][:, cols].bitcast(FP8X4), rhs_scale=z_s[0][:, cols], start=False, stop=False)
+            return acc
+
+        def close_scores(acc, tiles, j0, width, engine):
+            cols = slice(j0, j0 + width)
+            for k, n in enumerate(tiles):
+                ncols = slice(N + P * n, N + P * (n + 1))
+                nc.tensor.matmul_mx(out=acc[:, width * k:width * (k + 1)], lhsT=w3_w[:, ncols].bitcast(FP8X4), lhsT_scale=w3_s[:, ncols],
+                                    rhs=z_w[1][:, cols].bitcast(FP8X4), rhs_scale=z_s[1][:, cols], start=False, stop=(k == len(tiles) - 1))
+            staged = ring.tile([P, len(tiles), width], F32, name="staged", tag="staged", bufs=6)
+            src = acc[:, 0:len(tiles) * width].rearrange("p (k j) -> p k j", k=len(tiles))
+            if engine == "v":
+                nc.vector.tensor_copy(out=staged[:], in_=src)
+            else:
+                nc.scalar.copy(out=staged[:], in_=src)
+            nc.sync.dma_start(out=out[P * tiles[0]:P * (tiles[-1] + 1), cols].rearrange("(k p) j -> p k j", k=len(tiles)), in_=staged[:])
+
+        def new_h(s):
+            tag = "h_last" if s == 7 else "h_odd" if s % 2 else "h_even"
+            return keep.tile([P, S], F32, name="h%d" % s, tag=tag, align_bytes=64)[:]
+
+        pick_words(0)
+        pick_scales(0, "v_s0")
+        pick_words(1)
+        quantize_w1(0, 0, "grouped_first")
+        pick_scales(1, "grouped_first")
+        w3_raw1 = keep.tile([P, 4, N], F32, name="w3_raw1", tag="table", align_bytes=64)
+        nc.sync.dma_start(out=w3_raw1[:], in_=w3[HALF:H, :].rearrange("(p i) n -> p i n", i=4))
+        quantize_w1(0, 1, "grouped")
+        first_stage(0, new_h(0))
+        first_stage(1, new_h(1))
+        gate0 = [keep.tile([P, 4, HALF], F32, name="gate0_%d" % half, tag="gate_%d" % half, align_bytes=64) for half in range(2)]
+        place(0, 2)
+        heat_terms(0, gate0)
+        first_stage(2, new_h(2))
+        quantize_w1(1, 0, "grouped")
+        quantize_w1(1, 1, "late_page")
+        pages.append(keep.tile([P, T2], F32, name="page3", tag="late_page", align_bytes=64))
+        heat_terms(1, gate0)
+        heat_terms(2, gate0)
+        place(1)
+        heat_terms(3, gate0)
+        first_stage(3, new_h(3))
+        nc.gpsimd.memset(pages[3][:], 0.0)
+        place(2)
+        first_stage(4, new_h(4))
+        place(3)
+        w3_grouped = keep.tile([P, 2 * N, 4], BF16, name="w3_grouped", tag="w3_grouped", align_bytes=64)
+        scale_heat(0)
+        round_w3(w3_raw0, 0)
+        round_w3(w3_raw1, 1)
+
+        x = keep.tile([P, 4, S], F32, name="x0", tag="h_odd", align_bytes=64)
+        read_pages(x, gate0, 0, HALF)
+        w3_w = keep.tile([P, 2 * N], U32, name="w3_w", tag="gate_0", align_bytes=64)
+        for third in range(3):
+            cols = slice(HALF * third, HALF * (third + 1))
+            nc.vector.quantize_mx(out=w3_w[:, cols].bitcast(FP8X4), scales=w3_s[:, cols], in_=w3_grouped[:, cols, :].rearrange("p n t -> p (n t)"))
+        read_pages(x, gate0, HALF, HALF, (3, 2, 1, 0))
+
+        late = keep.tile([P, 5, S], F32, name="gate1", tag="gate_1", align_bytes=64)
+        gate1 = [late[:, 0:4, HALF * half:HALF * (half + 1)] for half in range(2)]
+        first_stage(5, late[:, 4, :])
+        place(4)
+        heat_terms(4, gate1)
+        heat_terms(5, gate1)
+        first_stage(6, new_h(6))
+        heat_terms(6, gate1)
+        heat_terms(7, gate1)
+        place(5)
+        first_stage(7, new_h(7))
+        z0 = [finish_z(0, x, HALF * half, HALF, "pe") for half in range(2)]
+        scale_heat(1)
+        place(6)
+        z_w[0] = keep.tile([P, S], U32, name="z_w0", tag="h_even", align_bytes=64)
+        for half in range(2):
+            quantize_z(0, z0[half], HALF * half, HALF)
+        place(7)
+
+        x = keep.tile([P, 4, S], F32, name="x1", tag="h_last", align_bytes=64)
+        starts = [sum(c[0] for c in TAIL[:k]) for k in range(len(TAIL))]
+        groups = [[list(range(6))[g * 6 // len(c[2]):(g + 1) * 6 // len(c[2])] for g in range(len(c[2]))] for c in TAIL]
+        opened = {}
+        busy = set()
+
+        def open_what_fits(k):
+            for c in range(len(TAIL)):
+                for g, number in enumerate(TAIL[c][2]):
+                    turning = number in (4, 5, 6) and any(later[1] == "pe" for later in TAIL[k:])
+                    if (c, g) not in opened and number not in busy and not turning:
+                        opened[c, g] = open_scores(number, groups[c][g], starts[c], TAIL[c][0])
+                        busy.add(number)
+
+        open_what_fits(0)
+        for c, (width, road, numbers, engines) in enumerate(TAIL):
+            read_pages(x, gate1, starts[c], width)
+            quantize_z(1, finish_z(1, x, starts[c], width, road), starts[c], width)
+            open_what_fits(c + 1)
+            for g, number in enumerate(numbers):
+                close_scores(opened[c, g], groups[c][g], starts[c], width, engines[g])
+                busy.remove(number)
+            open_what_fits(c + 1)

@@ -19,8 +19,8 @@ ACT = mybir.ActivationFunctionType
 
 P = 128
 HALF = 512
-POOL = True
-TAIL = [(256, "pe", [0, 1, 2], "sss"), (256, "v", [3, 7, 4], "sss"), (256, "v", [5, 6, 0], "sss"), (128, "v", [1, 2], "ss"), (128, "v", [3, 7], "sv")]
+DRIFT = 8
+TAIL = [(256, "pe", [0, 1, 2], "sss"), (256, "v", [6, 7, 3], "sss"), (256, "v", [4, 5, 0], "sss"), (128, "v", [1, 2], "ss"), (128, "v", [6, 7], "sv")]
 
 
 def tile_list_roast_phase_scores_kernel(tc, tab_words, tab_scales, offs, w1, b1, w2_words, w2_scales, wgs, offs2, wgt,
@@ -28,7 +28,6 @@ def tile_list_roast_phase_scores_kernel(tc, tab_words, tab_scales, offs, w1, b1,
     nc = tc.nc
     with ExitStack() as ctx:
         keep = ctx.enter_context(tc.tile_pool(name="keep", bufs=1))
-        ring = ctx.enter_context(tc.tile_pool(name="ring", bufs=2))
         psum = ctx.enter_context(tc.psum_pool(name="psum", bufs=1))
 
         def bank(number, name):
@@ -41,10 +40,10 @@ def tile_list_roast_phase_scores_kernel(tc, tab_words, tab_scales, offs, w1, b1,
         list1 = keep.tile([P, S // 16], U16, name="list1")
         list2 = keep.tile([P, S // 16], U16, name="list2")
         list3 = keep.tile([P, S // 16], U16, name="list3")
-        tab_s = keep.tile([P, T], U8, name="tab_s", align_bytes=64)
+        tab_s = keep.tile([P, T], U8, name="tab_s", tag="tab_s", align_bytes=64)
         w2_s_raw = keep.tile([P, H], U8, name="w2_s_raw", align_bytes=64)
         w4_s = keep.tile([P, N], U8, name="w4_s", align_bytes=64)
-        nc.vector.memset(w2_s_raw[:].bitcast(I32), 0)
+        nc.gpsimd.memset(w2_s_raw[:].bitcast(I32), 0)
         nc.vector.memset(tab_s[:].bitcast(I32), 0)
         nc.vector.memset(w4_s[:].bitcast(I32), 0)
 
@@ -52,7 +51,7 @@ def tile_list_roast_phase_scores_kernel(tc, tab_words, tab_scales, offs, w1, b1,
         nc.vector.memset(warm[:], 0.0)
         nc.scalar.activation(warm[:], warm[:], ACT.Sigmoid)
 
-        w2_raw = keep.tile([P, 2 * H], U8, name="w2_raw", align_bytes=64)
+        w2_raw = keep.tile([P, 2 * H], U8, name="w2_raw", tag="w2_raw", align_bytes=64)
         nc.sync.dma_start(out=w2_raw[:].bitcast(I32), in_=w2_words[0].bitcast(I32))
         tab_w = keep.tile([P, T], I32, name="tab_w", tag="table", align_bytes=64)
         nc.sync.dma_start(out=tab_w[:], in_=tab_words[0].rearrange("p t i -> p (t i)").bitcast(I32))
@@ -61,7 +60,7 @@ def tile_list_roast_phase_scores_kernel(tc, tab_words, tab_scales, offs, w1, b1,
         load_scale_rows(nc.sync, tab_s, tab_scales[0])
 
         w1_raw = [keep.tile([P, 4, HALF], F32, name="w1_raw0", tag="gate_0", align_bytes=64),
-                  keep.tile([P, 4, HALF], F32, name="w1_raw1", tag="w3_grouped", align_bytes=64)]
+                  keep.tile([P, 4, HALF], F32, name="w1_raw1", tag="gate_late", align_bytes=64)]
         nc.sync.dma_start(out=w1_raw[0][:], in_=w1[:, 0:HALF].rearrange("(p t) c -> p t c", t=4))
         b1_sb = keep.tile([P, 2, 4], F32, name="b1_sb")
         nc.sync.dma_start(out=b1_sb[:], in_=b1.rearrange("(b p i) -> p b i", b=2, i=4))
@@ -87,7 +86,7 @@ def tile_list_roast_phase_scores_kernel(tc, tab_words, tab_scales, offs, w1, b1,
         ident = keep.tile([P, P], F32, name="ident")
         make_identity(nc, ident[:])
 
-        pages = [keep.tile([P, T2], F32, name="page%d" % i) for i in range(3)]
+        pages = [keep.tile([P, T2], F32, name="page%d" % i) for i in range(2)]
         for page in pages:
             nc.vector.memset(page[:], 0.0)
 
@@ -107,97 +106,139 @@ def tile_list_roast_phase_scores_kernel(tc, tab_words, tab_scales, offs, w1, b1,
             v_s[half] = keep.tile([P, HALF], U8, name="v_s%d" % half, tag=tag, align_bytes=64)
             nc.vector.tensor_copy(v_s[half][:], tab_s[:].indirect(list1[:, 32 * half:32 * (half + 1)]))
 
-        w1_w = keep.tile([P, 8 * P], U32, name="w1_w", align_bytes=64)
+        w1_w = {0: keep.tile([P, HALF], U32, name="w1_w0", align_bytes=64)}
         w1_s = keep.tile([P, 8 * P], U8, name="w1_s", align_bytes=64)
 
-        def quantize_w1(b, u, tag):
-            grouped = keep.tile([P, 2, P, 4], BF16, name="w1_grouped", tag=tag, align_bytes=64)
-            nc.scalar.copy(out=grouped[:].rearrange("p e q t -> p q t e"),
+        def round_w1(b, u, grouped):
+            nc.scalar.copy(out=grouped.rearrange("p e q t -> p q t e"),
                            in_=w1_raw[b][:].rearrange("p t (q i) -> p q t i", i=4)[:, :, :, 2 * u:2 * u + 2])
-            cols = slice((4 * b + 2 * u) * P, (4 * b + 2 * u + 2) * P)
-            nc.vector.quantize_mx(out=w1_w[:, cols].bitcast(FP8X4), scales=w1_s[:, cols], in_=grouped[:].rearrange("p e q t -> p (e q t)"))
 
+        def quantize_w1_first(u, tag):
+            grouped = keep.tile([P, 2, P, 4], BF16, name="w1_grouped", tag=tag, align_bytes=64)
+            round_w1(0, u, grouped[:])
+            cols = slice(2 * P * u, 2 * P * (u + 1))
+            nc.vector.quantize_mx(out=w1_w[0][:, cols].bitcast(FP8X4), scales=w1_s[:, cols], in_=grouped[:].rearrange("p e q t -> p (e q t)"))
+
+        w3_w = {}
         w3_s = keep.tile([P, 2 * N], U8, name="w3_s", align_bytes=64)
 
-        def round_w3(raw, b):
-            for third in range(3):
-                cols = slice(256 * third, 256 * (third + 1))
-                nc.scalar.copy(out=w3_grouped[:, N * b + cols.start:N * b + cols.stop, :].rearrange("p (c e) t -> p c t e", e=4),
-                               in_=raw[:, :, cols].rearrange("p t (c e) -> p c t e", e=4))
+        def round_w3(raw, grouped, third):
+            cols = slice(256 * third, 256 * (third + 1))
+            nc.scalar.copy(out=grouped[:, cols, :].rearrange("p (c e) t -> p c t e", e=4), in_=raw[:, :, cols].rearrange("p t (c e) -> p c t e", e=4))
+
+        def quantize_w3(grouped, b, tag):
+            w3_w[b] = keep.tile([P, N], U32, name="w3_w%d" % b, tag=tag, align_bytes=64)
+            for c0, c1 in ((0, HALF), (HALF, N)):
+                nc.vector.quantize_mx(out=w3_w[b][:, c0:c1].bitcast(FP8X4), scales=w3_s[:, N * b + c0:N * b + c1],
+                                      in_=grouped[:, c0:c1, :].rearrange("p n t -> p (n t)"))
 
         h_tiles = {}
 
-        def first_stage(s, h):
+        products = {}
+        h_tag = ["h_even", "h_odd", "h_even", "h_odd", "h_even", "tab_s", "h_even", "h_last"]
+        held_back = {0: "page3", 2: "w1_w1", 4: "x0_late", 5: "w3_w0", 7: "z_w0"}
+        stage = keep.tile([P, S + 8 * DRIFT], F32, name="stage")
+
+        def first_products(s):
             b, i = divmod(s, 4)
-            wcols = slice(P * s, P * (s + 1))
-            biased = ring.tile([P, S], F32, name="biased", tag="biased")
-            h_tiles[s] = h
-            for half in range(2):
+            for half in ((0, 1) if s == 0 else (1, 0)):
                 cols = slice(HALF * half, HALF * (half + 1))
-                read1 = bank(half, "read1")
-                nc.tensor.matmul_mx(out=read1[:], lhsT=w1_w[:, wcols].bitcast(FP8X4), lhsT_scale=w1_s[:, wcols],
+                if half == 0:
+                    biased = keep.tile([P, HALF], F32, name="biased", tag=held_back.get(s, "biased"), align_bytes=64)[:]
+                else:
+                    biased = stage[:, HALF + DRIFT * s:S + DRIFT * s]
+                read1 = bank(7 if s < 2 and half == 1 else 2, "read1")
+                nc.tensor.matmul_mx(out=read1[:], lhsT=w1_w[b][:, P * i:P * (i + 1)].bitcast(FP8X4), lhsT_scale=w1_s[:, P * s:P * (s + 1)],
                                     rhs=v_w[:, cols].bitcast(FP8X4), rhs_scale=v_s[half][:], start=True, stop=True)
-                read2 = bank(2 + half, "read2")
+                read2 = bank(half, "read2")
                 nc.tensor.matmul_mx(out=read2[:], lhsT=w2_w[:, b, i].rearrange("p q e -> p (q e)").bitcast(FP4X4), lhsT_scale=w2_s[:, b, i],
                                     rhs=v_w[:, cols].bitcast(FP8X4), rhs_scale=v_s[half][:], start=True, stop=True)
-                nc.scalar.activation(biased[:, cols], read1[:], ACT.Identity, bias=b1_sb[:, b, i:i + 1])
-                nc.vector.tensor_tensor(h[:, cols], read2[:], biased[:, cols], ALU.max)
-                if POOL:
-                    nc.gpsimd.tensor_tensor(h[:, cols], h[:, cols], wgs_sb[:, cols], ALU.mult)
+                nc.scalar.activation(biased, read1[:], ACT.Identity, bias=b1_sb[:, b, i:i + 1])
+                products[s, half] = (read2, biased)
+
+        def larger(s):
+            h_tiles[s] = keep.tile([P, S], F32, name="h%d" % s, tag=h_tag[s], align_bytes=64)
+            for half in range(2):
+                read2, biased = products[s, half]
+                nc.vector.tensor_tensor(h_tiles[s][:, HALF * half:HALF * (half + 1)], read2[:], biased, ALU.max)
 
         def place(s, parts=1):
             h = h_tiles[s]
             for part in range(parts):
                 cols = slice(S // parts * part, S // parts * (part + 1))
                 window = pages[s % 4][:].indirect(list2[:, cols.start // 16:cols.stop // 16])
-                if POOL:
-                    nc.vector.tensor_copy(window, h[:, cols])
-                else:
-                    nc.vector.tensor_tensor(window, h[:, cols], wgs_sb[:, cols], ALU.mult)
+                nc.vector.tensor_tensor(window, h[:, cols], wgs_sb[:, cols], ALU.mult)
 
-        def heat_terms(s, gate_halves):
-            b, i = divmod(s, 4)
+        wgt_turned = keep.tile([P, 8, 8], F32, name="wgt_turned")
+
+        def turn_wgt():
             for half in range(2):
-                cols = slice(HALF * half, HALF * (half + 1))
-                gate = gate_halves[half][:, i, :]
-                nc.scalar.activation(gate, heat_sb[b][:, i, cols], ACT.Sigmoid)
-                eng = nc.gpsimd if POOL else nc.vector
-                eng.tensor_tensor(gate, gate, wgt_sb[:, cols], ALU.mult)
+                turned = bank(3 + half, "wgt_bank")
+                for k in range(4):
+                    c0 = HALF * half + P * k
+                    nc.tensor.transpose(turned[:, P * k:P * (k + 1)], wgt_sb[:, c0:c0 + P], ident[:])
+                nc.scalar.copy(out=wgt_turned[:, 4 * half:4 * half + 4, :], in_=turned[:].rearrange("j (k g q) -> j k g q", k=4, g=8)[:, :, :, 0])
 
-        def scale_heat(b):
+        def turned_gate(b, blk, gate_halves, tag, number):
+            half, g0 = divmod(P * blk, HALF)
+            turned = bank(number, "heat_turned")
             for i in range(4):
-                nc.scalar.activation(heat_sb[b][:, i, :], heat_sb[b][:, i, :], ACT.Copy, scale=hg_sb[:, b, i:i + 1])
+                nc.tensor.transpose(turned[:, P * i:P * (i + 1)], heat_sb[b][:, i, P * blk:P * (blk + 1)], ident[:])
+            opened = keep.tile([P, 4, P], F32, name="opened", tag=tag, align_bytes=64)
+            nc.scalar.activation(opened[:].rearrange("j i p -> j (i p)"), turned[:], ACT.Sigmoid)
+            for g in range(8):
+                part = opened[:, :, 16 * g:16 * (g + 1)]
+                nc.scalar.activation(part, part, ACT.Copy, scale=wgt_turned[:, blk, g:g + 1])
+            back = bank(5 + blk % 2, "gate_back")
+            for i in range(4):
+                nc.tensor.transpose(back[:, P * i:P * (i + 1)], opened[:, i, :], ident[:])
+            nc.scalar.copy(out=gate_halves[half][:, :, g0:g0 + P], in_=back[:].rearrange("p (i j) -> p i j", i=4))
+
+        def plain_gate(s, gate_halves, engine):
+            b, i = divmod(s, 4)
+            if s == 4:
+                opened = keep.tile([P, HALF], F32, name="opened_half", tag="gate_1", align_bytes=64)[:]
+            else:
+                opened = stage[:, DRIFT * (s + 1):HALF + DRIFT * (s + 1)]
+            nc.scalar.activation(opened, heat_sb[b][:, i, HALF:S], ACT.Sigmoid)
+            engine.tensor_tensor(gate_halves[1][:, i, :], opened, wgt_sb[:, HALF:S], ALU.mult)
+
+        def scale_heat(s, half):
+            b, i = divmod(s, 4)
+            part = heat_sb[b][:, i, HALF * half:HALF * (half + 1)]
+            nc.scalar.activation(part, part, ACT.Copy, scale=hg_sb[:, b, i:i + 1])
 
         z_w = {1: keep.tile([P, S], U32, name="z_w1", align_bytes=64)}
         z_s = [keep.tile([P, S], U8, name="z_s%d" % b, align_bytes=64) for b in range(2)]
 
-        def read_pages(x, gate_halves, j0, width, order=(0, 1, 2, 3)):
+        def read_pages(x, gate_halves, j0, width):
             half, g0 = divmod(j0, HALF)
-            for i in order:
-                nc.vector.tensor_tensor(x[:, i, j0:j0 + width], pages[i][:].indirect(list3[:, j0 // 16:(j0 + width) // 16]),
+            for i in range(4):
+                nc.vector.tensor_tensor(x[:, i, :], pages[i][:].indirect(list3[:, j0 // 16:(j0 + width) // 16]),
                                         gate_halves[half][:, i, g0:g0 + width], ALU.mult)
 
-        def finish_z(b, x, j0, width, road):
-            z = ring.tile([P, width, 4], BF16, name="z", tag="z", align_bytes=64)
+        def finish_z(b, x, j0, width, road, z_tag, last_tag=None):
+            z = keep.tile([P, width, 4], BF16, name="z", tag=z_tag, align_bytes=64)
             hh = heat_sb[b]
             cols = slice(j0, j0 + width)
             if road == "v":
-                nc.vector.tensor_tensor(z[:].rearrange("p (c e) i -> p c i e", e=4), x[:, :, cols].rearrange("p i (c e) -> p c i e", e=4),
+                nc.vector.tensor_tensor(z[:].rearrange("p (c e) i -> p c i e", e=4), x.rearrange("p i (c e) -> p c i e", e=4),
                                         hh[:, :, cols].rearrange("p i (c e) -> p c i e", e=4), ALU.add)
             else:
                 z_words = z[:].rearrange("p j i -> p (j i)").bitcast(F32).rearrange("p (j u) -> p j u", u=2)
                 for pair in range(width // 256):
-                    back = bank(6, "back")
+                    back = bank(5 + pair % 2, "back")
                     for blk in range(2):
                         c0 = j0 + 256 * pair + P * blk
-                        turned = bank(4 + blk, "turned")
+                        turned = bank(3 + blk, "turned")
                         for i in range(4):
                             nc.tensor.matmul(turned[:, P * i:P * (i + 1)], lhsT=hh[:, i, c0:c0 + P], rhs=ident[:],
                                              is_transpose=True, start=(i == 0), stop=False)
                         for i in range(4):
-                            nc.tensor.matmul(turned[:, P * i:P * (i + 1)], lhsT=x[:, i, c0:c0 + P], rhs=ident[:],
+                            nc.tensor.matmul(turned[:, P * i:P * (i + 1)], lhsT=x[:, i, c0 - j0:c0 - j0 + P], rhs=ident[:],
                                              is_transpose=True, start=False, stop=(i == 3))
-                        z_turned = ring.tile([P, 2, P, 2], BF16, name="z_turned", tag="z_turned")
+                        tag = last_tag if last_tag and c0 + P == j0 + width else "z_turned%d" % blk
+                        z_turned = keep.tile([P, 2, P, 2], BF16, name="z_turned", tag=tag, align_bytes=64)
                         nc.scalar.copy(out=z_turned[:], in_=turned[:].rearrange("j (u e p) -> j u p e", u=2, e=2))
                         words = z_turned[:].rearrange("j u p e -> j (u p e)").bitcast(F32)
                         for u in range(2):
@@ -218,17 +259,17 @@ def tile_list_roast_phase_scores_kernel(tc, tab_words, tab_scales, offs, w1, b1,
                 ncols = slice(P * n, P * (n + 1))
                 nc.tensor.matmul_mx(out=acc[:, width * k:width * (k + 1)], lhsT=w4_w[:, ncols].bitcast(FP8X4), lhsT_scale=w4_s[:, ncols],
                                     rhs=v_w[:, cols].bitcast(FP8X4), rhs_scale=v_s[half][:, g0:g0 + width], start=(k == 0), stop=False)
-                nc.tensor.matmul_mx(out=acc[:, width * k:width * (k + 1)], lhsT=w3_w[:, ncols].bitcast(FP8X4), lhsT_scale=w3_s[:, ncols],
+                nc.tensor.matmul_mx(out=acc[:, width * k:width * (k + 1)], lhsT=w3_w[0][:, ncols].bitcast(FP8X4), lhsT_scale=w3_s[:, ncols],
                                     rhs=z_w[0][:, cols].bitcast(FP8X4), rhs_scale=z_s[0][:, cols], start=False, stop=False)
             return acc
 
-        def close_scores(acc, tiles, j0, width, engine):
+        def close_scores(acc, tiles, j0, width, engine, tag):
             cols = slice(j0, j0 + width)
             for k, n in enumerate(tiles):
-                ncols = slice(N + P * n, N + P * (n + 1))
-                nc.tensor.matmul_mx(out=acc[:, width * k:width * (k + 1)], lhsT=w3_w[:, ncols].bitcast(FP8X4), lhsT_scale=w3_s[:, ncols],
+                nc.tensor.matmul_mx(out=acc[:, width * k:width * (k + 1)], lhsT=w3_w[1][:, P * n:P * (n + 1)].bitcast(FP8X4),
+                                    lhsT_scale=w3_s[:, N + P * n:N + P * (n + 1)],
                                     rhs=z_w[1][:, cols].bitcast(FP8X4), rhs_scale=z_s[1][:, cols], start=False, stop=(k == len(tiles) - 1))
-            staged = ring.tile([P, len(tiles), width], F32, name="staged", tag="staged", bufs=6)
+            staged = keep.tile([P, len(tiles), width], F32, name="staged", tag=tag, align_bytes=64)
             src = acc[:, 0:len(tiles) * width].rearrange("p (k j) -> p k j", k=len(tiles))
             if engine == "v":
                 nc.vector.tensor_copy(out=staged[:], in_=src)
@@ -236,88 +277,127 @@ def tile_list_roast_phase_scores_kernel(tc, tab_words, tab_scales, offs, w1, b1,
                 nc.scalar.copy(out=staged[:], in_=src)
             nc.sync.dma_start(out=out[P * tiles[0]:P * (tiles[-1] + 1), cols].rearrange("(k p) j -> p k j", k=len(tiles)), in_=staged[:])
 
-        def new_h(s):
-            tag = "h_last" if s == 7 else "h_odd" if s % 2 else "h_even"
-            return keep.tile([P, S], F32, name="h%d" % s, tag=tag, align_bytes=64)[:]
-
         pick_words(0)
         pick_scales(0, "v_s0")
         pick_words(1)
-        quantize_w1(0, 0, "grouped_first")
+        quantize_w1_first(0, "grouped_first")
         pick_scales(1, "grouped_first")
         w3_raw1 = keep.tile([P, 4, N], F32, name="w3_raw1", tag="table", align_bytes=64)
         nc.sync.dma_start(out=w3_raw1[:], in_=w3[HALF:H, :].rearrange("(p i) n -> p i n", i=4))
-        quantize_w1(0, 1, "grouped")
-        first_stage(0, new_h(0))
-        first_stage(1, new_h(1))
+        quantize_w1_first(1, "page2")
+        first_products(0)
+        larger(0)
+        for i in (2, 3):
+            pages.append(keep.tile([P, T2], F32, name="page%d" % i, tag="page%d" % i, align_bytes=64))
+            nc.gpsimd.memset(pages[i][:], 0.0)
         gate0 = [keep.tile([P, 4, HALF], F32, name="gate0_%d" % half, tag="gate_%d" % half, align_bytes=64) for half in range(2)]
-        place(0, 2)
-        heat_terms(0, gate0)
-        first_stage(2, new_h(2))
-        quantize_w1(1, 0, "grouped")
-        quantize_w1(1, 1, "late_page")
-        pages.append(keep.tile([P, T2], F32, name="page3", tag="late_page", align_bytes=64))
-        heat_terms(1, gate0)
-        heat_terms(2, gate0)
+
+        place(0)
+        turn_wgt()
+        turned_gate(0, 0, gate0, h_tag[1], 0)
+        first_products(1)
+        plain_gate(0, gate0, nc.gpsimd)
+        larger(1)
+
         place(1)
-        heat_terms(3, gate0)
-        first_stage(3, new_h(3))
-        nc.gpsimd.memset(pages[3][:], 0.0)
+        turned_gate(0, 1, gate0, h_tag[2], 0)
+        first_products(2)
+        plain_gate(1, gate0, nc.gpsimd)
+        w1_grouped = keep.tile([P, 4, P, 4], BF16, name="w1_grouped", tag="w3_grouped", align_bytes=64)
+        for u in range(2):
+            round_w1(1, u, w1_grouped[:, 2 * u:2 * u + 2])
+        larger(2)
+        w1_w[1] = keep.tile([P, HALF], U32, name="w1_w1", tag="w1_w1", align_bytes=64)
+        nc.vector.quantize_mx(out=w1_w[1][:].bitcast(FP8X4), scales=w1_s[:, HALF:S], in_=w1_grouped[:].rearrange("p i q t -> p (i q t)"))
+
         place(2)
-        first_stage(4, new_h(4))
+        turned_gate(0, 2, gate0, h_tag[3], 0)
+        first_products(3)
+        plain_gate(2, gate0, nc.gpsimd)
+        w3_grouped = keep.tile([P, N, 4], BF16, name="w3_grouped0", tag="w3_grouped", align_bytes=64)
+        round_w3(w3_raw0, w3_grouped, 0)
+        scale_heat(0, 1)
+        late = keep.tile([P, 4, S], F32, name="gate1", tag="gate_late", align_bytes=64)
+        gate1 = [late[:, :, HALF * half:HALF * (half + 1)] for half in range(2)]
+        turned_gate(1, 0, gate1, "opened", 7)
+        larger(3)
+
         place(3)
-        w3_grouped = keep.tile([P, 2 * N, 4], BF16, name="w3_grouped", tag="w3_grouped", align_bytes=64)
-        scale_heat(0)
-        round_w3(w3_raw0, 0)
-        round_w3(w3_raw1, 1)
+        turned_gate(0, 3, gate0, h_tag[4], 0)
+        first_products(4)
+        plain_gate(3, gate0, nc.gpsimd)
+        round_w3(w3_raw0, w3_grouped, 1)
+        scale_heat(1, 1)
+        turned_gate(1, 1, gate1, "opened", 7)
+        larger(4)
 
-        x = keep.tile([P, 4, S], F32, name="x0", tag="h_odd", align_bytes=64)
-        read_pages(x, gate0, 0, HALF)
-        w3_w = keep.tile([P, 2 * N], U32, name="w3_w", tag="gate_0", align_bytes=64)
-        for third in range(3):
-            cols = slice(HALF * third, HALF * (third + 1))
-            nc.vector.quantize_mx(out=w3_w[:, cols].bitcast(FP8X4), scales=w3_s[:, cols], in_=w3_grouped[:, cols, :].rearrange("p n t -> p (n t)"))
-        read_pages(x, gate0, HALF, HALF, (3, 2, 1, 0))
+        x = [keep.tile([P, 4, HALF], F32, name="x0_%d" % half, tag=tag, align_bytes=64)[:] for half, tag in enumerate(("h_odd", "x0_late"))]
+        read_pages(x[0], gate0, 0, HALF)
+        read_pages(x[1], gate0, HALF, HALF)
+        first_products(5)
+        for i in range(4):
+            scale_heat(i, 0)
+        scale_heat(2, 1)
+        scale_heat(3, 1)
+        round_w3(w3_raw0, w3_grouped, 2)
 
-        late = keep.tile([P, 5, S], F32, name="gate1", tag="gate_1", align_bytes=64)
-        gate1 = [late[:, 0:4, HALF * half:HALF * (half + 1)] for half in range(2)]
-        first_stage(5, late[:, 4, :])
         place(4)
-        heat_terms(4, gate1)
-        heat_terms(5, gate1)
-        first_stage(6, new_h(6))
-        heat_terms(6, gate1)
-        heat_terms(7, gate1)
+        plain_gate(4, gate1, nc.gpsimd)
+        z0 = [finish_z(0, x[0], 0, HALF, "pe", "z_a", h_tag[5])]
+        larger(5)
+        quantize_w3(w3_grouped, 0, "w3_w0")
+
         place(5)
-        first_stage(7, new_h(7))
-        z0 = [finish_z(0, x, HALF * half, HALF, "pe") for half in range(2)]
-        scale_heat(1)
+        first_products(6)
+        plain_gate(5, gate1, nc.gpsimd)
+        w3_grouped = keep.tile([P, N, 4], BF16, name="w3_grouped1", tag="w3_grouped", align_bytes=64)
+        z0.append(finish_z(0, x[1], HALF, HALF, "pe", "z_b", h_tag[6]))
+        round_w3(w3_raw1, w3_grouped, 0)
+        larger(6)
+
         place(6)
-        z_w[0] = keep.tile([P, S], U32, name="z_w0", tag="h_even", align_bytes=64)
+        turned_gate(1, 2, gate1, h_tag[7], 0)
+        first_products(7)
+        plain_gate(6, gate1, nc.gpsimd)
+        round_w3(w3_raw1, w3_grouped, 1)
+        round_w3(w3_raw1, w3_grouped, 2)
+        larger(7)
+        z_w[0] = keep.tile([P, S], U32, name="z_w0", tag="z_w0", align_bytes=64)
         for half in range(2):
             quantize_z(0, z0[half], HALF * half, HALF)
-        place(7)
+        quantize_w3(w3_grouped, 1, "z_a")
 
-        x = keep.tile([P, 4, S], F32, name="x1", tag="h_last", align_bytes=64)
+        place(7)
+        plain_gate(7, gate1, nc.vector)
+        turned_gate(1, 3, gate1, "opened", 3)
+        for half in range(2):
+            for i in range(4):
+                scale_heat(4 + i, half)
+
+        x1 = keep.tile([P, 2, 4, 256], F32, name="x1", tag="h_last", align_bytes=64)
         starts = [sum(c[0] for c in TAIL[:k]) for k in range(len(TAIL))]
         groups = [[list(range(6))[g * 6 // len(c[2]):(g + 1) * 6 // len(c[2])] for g in range(len(c[2]))] for c in TAIL]
         opened = {}
+        stored = []
+        free_slots = ["gate_0", "h_odd", "x0_late", "table", "w3_grouped", "h_even", "tab_s", "gate_1", "opened", "biased", "w2_raw", "st0", "st1"]
         busy = set()
 
         def open_what_fits(k):
             for c in range(len(TAIL)):
                 for g, number in enumerate(TAIL[c][2]):
-                    turning = number in (4, 5, 6) and any(later[1] == "pe" for later in TAIL[k:])
+                    turning = number in (3, 4, 5) and any(later[1] == "pe" for later in TAIL[k:])
                     if (c, g) not in opened and number not in busy and not turning:
                         opened[c, g] = open_scores(number, groups[c][g], starts[c], TAIL[c][0])
                         busy.add(number)
 
         open_what_fits(0)
         for c, (width, road, numbers, engines) in enumerate(TAIL):
+            x = x1[:, c] if c < 2 else keep.tile([P, 4, width], F32, name="x_tail", tag="z_b", align_bytes=64)[:]
             read_pages(x, gate1, starts[c], width)
-            quantize_z(1, finish_z(1, x, starts[c], width, road), starts[c], width)
+            quantize_z(1, finish_z(1, x, starts[c], width, road, ["z_b", "z_turned1", "z_c0", "z_c1", "z_c0"][c]), starts[c], width)
             open_what_fits(c + 1)
             for g, number in enumerate(numbers):
-                close_scores(opened[c, g], groups[c][g], starts[c], width, engines[g])
+                close_scores(opened[c, g], groups[c][g], starts[c], width, engines[g], free_slots[len(stored)])
+                stored.append(number)
                 busy.remove(number)
             open_what_fits(c + 1)

@@ -4,7 +4,7 @@ import concourse.mybir as mybir
 from concourse.masks import make_identity
 
 K, T, S, T2, H, N = 512, 4096, 1024, 2048, 1024, 768
-FLOPS = 2 * K * H * S * 2 + 2 * H * N * S + 2 * K * N * S
+FLOPS = 2 * (2 * K * H * S) + 2 * H * N * S + 2 * K * N * S
 
 F32 = mybir.dt.float32
 BF16 = mybir.dt.bfloat16
@@ -19,132 +19,135 @@ ACT = mybir.ActivationFunctionType
 
 P = 128
 HALF = 512
+QUARTER = 256
+ROW_TILES = N // P
 DRIFT = 8
-TAIL = [(256, "pe", [0, 1, 2], "sss"), (256, "v", [6, 7, 3], "sss"), (256, "v", [4, 5, 0], "sss"), (128, "v", [1, 2], "ss"), (128, "v", [6, 7], "sv")]
+CHUNK_WIDTHS = [QUARTER, QUARTER, QUARTER, P, P]
 
 
 def tile_list_roast_phase_scores_kernel(tc, tab_words, tab_scales, offs, w1, b1, w2_words, w2_scales, wgs, offs2, wgt,
                                                   offs3, heat, hg, w3, w4_words, w4_scales, out):
     nc = tc.nc
     with ExitStack() as ctx:
-        keep = ctx.enter_context(tc.tile_pool(name="keep", bufs=1))
+        sbuf = ctx.enter_context(tc.tile_pool(name="sbuf", bufs=1))
         psum = ctx.enter_context(tc.psum_pool(name="psum", bufs=1))
+
+        def new_tile(shape, dtype, name, tag):
+            return sbuf.tile(shape, dtype, name=name, tag=tag, align_bytes=64)
 
         def bank(number, name):
             return psum.tile([P, HALF], F32, tag="bank%d" % number, name=name)
 
-        def load_scale_rows(queue, plane, rows):
+        def load_scale_rows(scales, rows):
             for quad in range(4):
-                queue.dma_start(out=plane[32 * quad:32 * quad + 4, :].bitcast(I32), in_=rows[4 * quad:4 * quad + 4, :].bitcast(I32))
+                nc.sync.dma_start(out=scales[32 * quad:32 * quad + 4, :].bitcast(I32), in_=rows[4 * quad:4 * quad + 4, :].bitcast(I32))
 
-        list1 = keep.tile([P, S // 16], U16, name="list1")
-        list2 = keep.tile([P, S // 16], U16, name="list2")
-        list3 = keep.tile([P, S // 16], U16, name="list3")
-        tab_s = keep.tile([P, T], U8, name="tab_s", tag="tab_s", align_bytes=64)
-        w2_s_raw = keep.tile([P, H], U8, name="w2_s_raw", align_bytes=64)
-        w4_s = keep.tile([P, N], U8, name="w4_s", align_bytes=64)
+        list1 = sbuf.tile([P, S // 16], U16, name="list1")
+        list2 = sbuf.tile([P, S // 16], U16, name="list2")
+        list3 = sbuf.tile([P, S // 16], U16, name="list3")
+        tab_s = new_tile([P, T], U8, "tab_s", "tab_s")
+        w2_s_raw = new_tile([P, H], U8, "w2_s_raw", "w2_s_raw")
+        w4_s = new_tile([P, N], U8, "w4_s", "w4_s")
         nc.gpsimd.memset(w2_s_raw[:].bitcast(I32), 0)
         nc.vector.memset(tab_s[:].bitcast(I32), 0)
         nc.vector.memset(w4_s[:].bitcast(I32), 0)
 
-        warm = keep.tile([P, 1], F32, name="warm")
-        nc.vector.memset(warm[:], 0.0)
-        nc.scalar.activation(warm[:], warm[:], ACT.Sigmoid)
-
-        w2_raw = keep.tile([P, 2 * H], U8, name="w2_raw", tag="w2_raw", align_bytes=64)
+        w2_raw = new_tile([P, 2 * H], U8, "w2_raw", "w2_raw")
         nc.sync.dma_start(out=w2_raw[:].bitcast(I32), in_=w2_words[0].bitcast(I32))
-        tab_w = keep.tile([P, T], I32, name="tab_w", tag="table", align_bytes=64)
+        tab_w = new_tile([P, T], I32, "tab_w", "table")
         nc.sync.dma_start(out=tab_w[:], in_=tab_words[0].rearrange("p t i -> p (t i)").bitcast(I32))
         nc.sync.dma_start(list1[:], offs)
-        load_scale_rows(nc.gpsimd, w2_s_raw, w2_scales[0])
-        load_scale_rows(nc.sync, tab_s, tab_scales[0])
+        load_scale_rows(tab_s, tab_scales[0])
 
-        w1_raw = [keep.tile([P, 4, HALF], F32, name="w1_raw0", tag="gate_0", align_bytes=64),
-                  keep.tile([P, 4, HALF], F32, name="w1_raw1", tag="gate_late", align_bytes=64)]
-        nc.sync.dma_start(out=w1_raw[0][:], in_=w1[:, 0:HALF].rearrange("(p t) c -> p t c", t=4))
-        b1_sb = keep.tile([P, 2, 4], F32, name="b1_sb")
+        w1_raw = [new_tile([P, 4, HALF], F32, "w1_raw0", "gate_0"), new_tile([P, 4, HALF], F32, "w1_raw1", "gate_late")]
+        for c0 in (0, QUARTER):
+            nc.sync.dma_start(out=w1_raw[0][:, :, c0:c0 + QUARTER], in_=w1[:, c0:c0 + QUARTER].rearrange("(p t) c -> p t c", t=4))
+        b1_sb = sbuf.tile([P, 2, 4], F32, name="b1_sb")
         nc.sync.dma_start(out=b1_sb[:], in_=b1.rearrange("(b p i) -> p b i", b=2, i=4))
-        wgs_sb = keep.tile([P, S], F32, name="wgs_sb")
+        load_scale_rows(w2_s_raw, w2_scales[0])
+        wgs_sb = sbuf.tile([P, S], F32, name="wgs_sb")
         nc.sync.dma_start(out=wgs_sb[:], in_=wgs)
         nc.sync.dma_start(list2[:], offs2)
-        heat_sb = [keep.tile([P, 4, S], F32, name="heat%d" % b) for b in range(2)]
-        wgt_sb = keep.tile([P, S], F32, name="wgt_sb")
+        heat_sb = [sbuf.tile([P, 4, S], F32, name="heat%d" % b) for b in range(2)]
+        wgt_sb = sbuf.tile([P, S], F32, name="wgt_sb")
         nc.sync.dma_start(out=wgt_sb[:], in_=wgt)
-        for u in range(2):
-            nc.sync.dma_start(out=heat_sb[0][:, 2 * u:2 * u + 2, :], in_=heat[0:HALF, :].rearrange("(p i) j -> p i j", i=4)[:, 2 * u:2 * u + 2, :])
-        hg_sb = keep.tile([P, 2, 4], F32, name="hg_sb")
+        for i0 in (0, 2):
+            nc.sync.dma_start(out=heat_sb[0][:, i0:i0 + 2, :], in_=heat[0:HALF, :].rearrange("(p i) j -> p i j", i=4)[:, i0:i0 + 2, :])
+        hg_sb = sbuf.tile([P, 2, 4], F32, name="hg_sb")
         nc.sync.dma_start(out=hg_sb[:], in_=hg.rearrange("(b p i) -> p b i", b=2, i=4))
         nc.sync.dma_start(list3[:], offs3)
         nc.sync.dma_start(out=w1_raw[1][:], in_=w1[:, HALF:H].rearrange("(p t) c -> p t c", t=4))
         nc.sync.dma_start(out=heat_sb[1][:], in_=heat[HALF:H, :].rearrange("(p i) j -> p i j", i=4))
-        w4_w = keep.tile([P, N], I32, name="w4_w", align_bytes=64)
+        w4_w = new_tile([P, N], I32, "w4_w", "w4_w")
         nc.sync.dma_start(out=w4_w[:], in_=w4_words[0].rearrange("p c i -> p (c i)").bitcast(I32))
-        load_scale_rows(nc.sync, w4_s, w4_scales[0])
-        w3_raw0 = keep.tile([P, 4, N], F32, name="w3_raw0", tag="h_last", align_bytes=64)
+        load_scale_rows(w4_s, w4_scales[0])
+        w3_raw0 = new_tile([P, 4, N], F32, "w3_raw0", "h_last")
         nc.sync.dma_start(out=w3_raw0[:], in_=w3[0:HALF, :].rearrange("(p i) n -> p i n", i=4))
 
-        ident = keep.tile([P, P], F32, name="ident")
+        ident = sbuf.tile([P, P], F32, name="ident")
         make_identity(nc, ident[:])
 
-        pages = [keep.tile([P, T2], F32, name="page%d" % i) for i in range(2)]
+        pages = [sbuf.tile([P, T2], F32, name="page%d" % i) for i in range(2)]
         for page in pages:
             nc.vector.memset(page[:], 0.0)
 
-        w2_w = keep.tile([P, 2, 4, P, 2], U8, name="w2_w", align_bytes=64)
-        w2_s = keep.tile([P, 2, 4, P], U8, name="w2_s", align_bytes=64)
+        w2_w = new_tile([P, 2, 4, P, 2], U8, "w2_w", "w2_w")
+        w2_s = new_tile([P, 2, 4, P], U8, "w2_s", "w2_s")
         for b in range(2):
             nc.vector.tensor_copy(out=w2_w[:, b], in_=w2_raw[:, 2 * HALF * b:2 * HALF * (b + 1)].rearrange("p (q i e) -> p i q e", i=4, e=2))
-        nc.vector.tensor_copy(out=w2_s[:], in_=w2_s_raw[:].rearrange("p (b q i) -> p b i q", b=2, i=4))
 
-        v_w = keep.tile([P, S], U32, name="v_w", align_bytes=64)
+        def deal_w2_scales(b):
+            nc.vector.tensor_copy(out=w2_s[:, b], in_=w2_s_raw[:, HALF * b:HALF * (b + 1)].rearrange("p (q i) -> p i q", i=4))
+
+        v_w = new_tile([P, S], U32, "v_w", "v_w")
         v_s = {}
 
         def pick_words(half):
             nc.vector.tensor_copy(v_w[:, HALF * half:HALF * (half + 1)], tab_w[:].bitcast(U32).indirect(list1[:, 32 * half:32 * (half + 1)]))
 
         def pick_scales(half, tag):
-            v_s[half] = keep.tile([P, HALF], U8, name="v_s%d" % half, tag=tag, align_bytes=64)
+            v_s[half] = new_tile([P, HALF], U8, "v_s%d" % half, tag)
             nc.vector.tensor_copy(v_s[half][:], tab_s[:].indirect(list1[:, 32 * half:32 * (half + 1)]))
 
-        w1_w = {0: keep.tile([P, HALF], U32, name="w1_w0", align_bytes=64)}
-        w1_s = keep.tile([P, 8 * P], U8, name="w1_s", align_bytes=64)
+        w1_w = {0: new_tile([P, HALF], U32, "w1_w0", "w1_w0")}
+        w1_s = new_tile([P, 8 * P], U8, "w1_s", "w1_s")
 
-        def round_w1(b, u, grouped):
-            nc.scalar.copy(out=grouped.rearrange("p e q t -> p q t e"),
-                           in_=w1_raw[b][:].rearrange("p t (q i) -> p q t i", i=4)[:, :, :, 2 * u:2 * u + 2])
+        def round_w1(b, u, grouped, q0, q1):
+            nc.scalar.copy(out=grouped.rearrange("p e q t -> p q t e")[:, q0:q1],
+                           in_=w1_raw[b][:].rearrange("p t (q i) -> p q t i", i=4)[:, q0:q1, :, 2 * u:2 * u + 2])
 
-        def quantize_w1_first(u, tag):
-            grouped = keep.tile([P, 2, P, 4], BF16, name="w1_grouped", tag=tag, align_bytes=64)
-            round_w1(0, u, grouped[:])
+        def quantize_w1_first_pass(u, q_ranges, tag):
+            grouped = new_tile([P, 2, P, 4], BF16, "w1_grouped", tag)
+            for q0, q1 in q_ranges:
+                round_w1(0, u, grouped[:], q0, q1)
             cols = slice(2 * P * u, 2 * P * (u + 1))
             nc.vector.quantize_mx(out=w1_w[0][:, cols].bitcast(FP8X4), scales=w1_s[:, cols], in_=grouped[:].rearrange("p e q t -> p (e q t)"))
 
         w3_w = {}
-        w3_s = keep.tile([P, 2 * N], U8, name="w3_s", align_bytes=64)
+        w3_s = new_tile([P, 2 * N], U8, "w3_s", "w3_s")
 
         def round_w3(raw, grouped, third):
-            cols = slice(256 * third, 256 * (third + 1))
+            cols = slice(QUARTER * third, QUARTER * (third + 1))
             nc.scalar.copy(out=grouped[:, cols, :].rearrange("p (c e) t -> p c t e", e=4), in_=raw[:, :, cols].rearrange("p t (c e) -> p c t e", e=4))
 
         def quantize_w3(grouped, b, tag):
-            w3_w[b] = keep.tile([P, N], U32, name="w3_w%d" % b, tag=tag, align_bytes=64)
+            w3_w[b] = new_tile([P, N], U32, "w3_w%d" % b, tag)
             for c0, c1 in ((0, HALF), (HALF, N)):
                 nc.vector.quantize_mx(out=w3_w[b][:, c0:c1].bitcast(FP8X4), scales=w3_s[:, N * b + c0:N * b + c1],
                                       in_=grouped[:, c0:c1, :].rearrange("p n t -> p (n t)"))
 
-        h_tiles = {}
-
-        products = {}
         h_tag = ["h_even", "h_odd", "h_even", "h_odd", "h_even", "tab_s", "h_even", "h_last"]
-        held_back = {0: "page3", 2: "w1_w1", 4: "x0_late", 5: "w3_w0", 7: "z_w0"}
-        stage = keep.tile([P, S + 8 * DRIFT], F32, name="stage")
+        follows_maximum = {0: "page3", 2: "w1_w1", 4: "x_late", 5: "w3_w0", 7: "z_w0"}
+        stage = sbuf.tile([P, S + 8 * DRIFT], F32, name="stage")
+        products = {}
+        h_tiles = {}
 
         def first_products(s):
             b, i = divmod(s, 4)
             for half in ((0, 1) if s == 0 else (1, 0)):
                 cols = slice(HALF * half, HALF * (half + 1))
                 if half == 0:
-                    biased = keep.tile([P, HALF], F32, name="biased", tag=held_back.get(s, "biased"), align_bytes=64)[:]
+                    biased = new_tile([P, HALF], F32, "biased", follows_maximum.get(s, "biased"))[:]
                 else:
                     biased = stage[:, HALF + DRIFT * s:S + DRIFT * s]
                 read1 = bank(7 if s < 2 and half == 1 else 2, "read1")
@@ -156,248 +159,251 @@ def tile_list_roast_phase_scores_kernel(tc, tab_words, tab_scales, offs, w1, b1,
                 nc.scalar.activation(biased, read1[:], ACT.Identity, bias=b1_sb[:, b, i:i + 1])
                 products[s, half] = (read2, biased)
 
-        def larger(s):
-            h_tiles[s] = keep.tile([P, S], F32, name="h%d" % s, tag=h_tag[s], align_bytes=64)
+        def take_maximum(s):
+            h_tiles[s] = new_tile([P, S], F32, "h%d" % s, h_tag[s])
             for half in range(2):
                 read2, biased = products[s, half]
                 nc.vector.tensor_tensor(h_tiles[s][:, HALF * half:HALF * (half + 1)], read2[:], biased, ALU.max)
 
-        def place(s, parts=1):
-            h = h_tiles[s]
-            for part in range(parts):
-                cols = slice(S // parts * part, S // parts * (part + 1))
-                window = pages[s % 4][:].indirect(list2[:, cols.start // 16:cols.stop // 16])
-                nc.vector.tensor_tensor(window, h[:, cols], wgs_sb[:, cols], ALU.mult)
+        def place(s):
+            nc.vector.tensor_tensor(pages[s % 4][:].indirect(list2[:]), h_tiles[s][:], wgs_sb[:], ALU.mult)
 
-        wgt_turned = keep.tile([P, 8, 8], F32, name="wgt_turned")
+        wgt_turned = sbuf.tile([P, 4, 8], F32, name="wgt_turned")
 
         def turn_wgt():
-            for half in range(2):
-                turned = bank(3 + half, "wgt_bank")
-                for k in range(4):
-                    c0 = HALF * half + P * k
-                    nc.tensor.transpose(turned[:, P * k:P * (k + 1)], wgt_sb[:, c0:c0 + P], ident[:])
-                nc.scalar.copy(out=wgt_turned[:, 4 * half:4 * half + 4, :], in_=turned[:].rearrange("j (k g q) -> j k g q", k=4, g=8)[:, :, :, 0])
+            turned = bank(3, "wgt_bank")
+            for blk in range(4):
+                nc.tensor.transpose(turned[:, P * blk:P * (blk + 1)], wgt_sb[:, P * blk:P * (blk + 1)], ident[:])
+            nc.scalar.copy(out=wgt_turned[:], in_=turned[:].rearrange("j (blk g q) -> j blk g q", blk=4, g=8)[:, :, :, 0])
 
-        def turned_gate(b, blk, gate_halves, tag, number):
-            half, g0 = divmod(P * blk, HALF)
-            turned = bank(number, "heat_turned")
+        def turned_gate(b, blk, gate, tag, bank_number):
+            cols = slice(P * blk, P * (blk + 1))
+            turned = bank(bank_number, "heat_turned")
             for i in range(4):
-                nc.tensor.transpose(turned[:, P * i:P * (i + 1)], heat_sb[b][:, i, P * blk:P * (blk + 1)], ident[:])
-            opened = keep.tile([P, 4, P], F32, name="opened", tag=tag, align_bytes=64)
-            nc.scalar.activation(opened[:].rearrange("j i p -> j (i p)"), turned[:], ACT.Sigmoid)
+                nc.tensor.transpose(turned[:, P * i:P * (i + 1)], heat_sb[b][:, i, cols], ident[:])
+            gate_turned = new_tile([P, 4, P], F32, "gate_turned", tag)
+            nc.scalar.activation(gate_turned[:].rearrange("j i p -> j (i p)"), turned[:], ACT.Sigmoid)
             for g in range(8):
-                part = opened[:, :, 16 * g:16 * (g + 1)]
-                nc.scalar.activation(part, part, ACT.Copy, scale=wgt_turned[:, blk, g:g + 1])
+                group = gate_turned[:, :, 16 * g:16 * (g + 1)]
+                nc.scalar.activation(group, group, ACT.Copy, scale=wgt_turned[:, blk, g:g + 1])
             back = bank(5 + blk % 2, "gate_back")
             for i in range(4):
-                nc.tensor.transpose(back[:, P * i:P * (i + 1)], opened[:, i, :], ident[:])
-            nc.scalar.copy(out=gate_halves[half][:, :, g0:g0 + P], in_=back[:].rearrange("p (i j) -> p i j", i=4))
+                nc.tensor.transpose(back[:, P * i:P * (i + 1)], gate_turned[:, i, :], ident[:])
+            nc.scalar.copy(out=gate[0][:, :, cols], in_=back[:].rearrange("p (i j) -> p i j", i=4))
 
-        def plain_gate(s, gate_halves, engine):
+        def plain_gate(s, gate, sigmoid, engine):
             b, i = divmod(s, 4)
-            if s == 4:
-                opened = keep.tile([P, HALF], F32, name="opened_half", tag="gate_1", align_bytes=64)[:]
-            else:
-                opened = stage[:, DRIFT * (s + 1):HALF + DRIFT * (s + 1)]
-            nc.scalar.activation(opened, heat_sb[b][:, i, HALF:S], ACT.Sigmoid)
-            engine.tensor_tensor(gate_halves[1][:, i, :], opened, wgt_sb[:, HALF:S], ALU.mult)
+            nc.scalar.activation(sigmoid, heat_sb[b][:, i, HALF:S], ACT.Sigmoid)
+            engine.tensor_tensor(gate[1][:, i, :], sigmoid, wgt_sb[:, HALF:S], ALU.mult)
+
+        def stage_left(s):
+            return stage[:, DRIFT * (s + 1):HALF + DRIFT * (s + 1)]
 
         def scale_heat(s, half):
             b, i = divmod(s, 4)
             part = heat_sb[b][:, i, HALF * half:HALF * (half + 1)]
             nc.scalar.activation(part, part, ACT.Copy, scale=hg_sb[:, b, i:i + 1])
 
-        z_w = {1: keep.tile([P, S], U32, name="z_w1", align_bytes=64)}
-        z_s = [keep.tile([P, S], U8, name="z_s%d" % b, align_bytes=64) for b in range(2)]
+        z_w = {1: new_tile([P, S], U32, "z_w1", "z_w1")}
+        z_s = [new_tile([P, S], U8, "z_s%d" % b, "z_s%d" % b) for b in range(2)]
 
-        def read_pages(x, gate_halves, j0, width):
+        def read_pages(x, gate, j0, width):
             half, g0 = divmod(j0, HALF)
             for i in range(4):
                 nc.vector.tensor_tensor(x[:, i, :], pages[i][:].indirect(list3[:, j0 // 16:(j0 + width) // 16]),
-                                        gate_halves[half][:, i, g0:g0 + width], ALU.mult)
+                                        gate[half][:, i, g0:g0 + width], ALU.mult)
 
-        def finish_z(b, x, j0, width, road, z_tag, last_tag=None):
-            z = keep.tile([P, width, 4], BF16, name="z", tag=z_tag, align_bytes=64)
-            hh = heat_sb[b]
-            cols = slice(j0, j0 + width)
-            if road == "v":
-                nc.vector.tensor_tensor(z[:].rearrange("p (c e) i -> p c i e", e=4), x.rearrange("p i (c e) -> p c i e", e=4),
-                                        hh[:, :, cols].rearrange("p i (c e) -> p c i e", e=4), ALU.add)
-            else:
-                z_words = z[:].rearrange("p j i -> p (j i)").bitcast(F32).rearrange("p (j u) -> p j u", u=2)
-                for pair in range(width // 256):
-                    back = bank(5 + pair % 2, "back")
-                    for blk in range(2):
-                        c0 = j0 + 256 * pair + P * blk
-                        turned = bank(3 + blk, "turned")
-                        for i in range(4):
-                            nc.tensor.matmul(turned[:, P * i:P * (i + 1)], lhsT=hh[:, i, c0:c0 + P], rhs=ident[:],
-                                             is_transpose=True, start=(i == 0), stop=False)
-                        for i in range(4):
-                            nc.tensor.matmul(turned[:, P * i:P * (i + 1)], lhsT=x[:, i, c0 - j0:c0 - j0 + P], rhs=ident[:],
-                                             is_transpose=True, start=False, stop=(i == 3))
-                        tag = last_tag if last_tag and c0 + P == j0 + width else "z_turned%d" % blk
-                        z_turned = keep.tile([P, 2, P, 2], BF16, name="z_turned", tag=tag, align_bytes=64)
-                        nc.scalar.copy(out=z_turned[:], in_=turned[:].rearrange("j (u e p) -> j u p e", u=2, e=2))
-                        words = z_turned[:].rearrange("j u p e -> j (u p e)").bitcast(F32)
-                        for u in range(2):
-                            nc.tensor.transpose(back[:, 256 * blk + P * u:256 * blk + P * (u + 1)], words[:, P * u:P * (u + 1)], ident[:])
-                    nc.scalar.copy(out=z_words[:, 256 * pair:256 * (pair + 1), :].rearrange("p (k j) u -> p k j u", k=2),
-                                   in_=back[:].rearrange("p (k u j) -> p k j u", k=2, u=2))
+        def add_heat_on_vector(b, x, j0, width, z_tag):
+            z = new_tile([P, width, 4], BF16, "z", z_tag)
+            nc.vector.tensor_tensor(z[:].rearrange("p (c e) i -> p c i e", e=4), x.rearrange("p i (c e) -> p c i e", e=4),
+                                    heat_sb[b][:, :, j0:j0 + width].rearrange("p i (c e) -> p c i e", e=4), ALU.add)
+            return z
+
+        def add_heat_by_transposes(b, x, j0, width, z_tag, last_tag):
+            z = new_tile([P, width, 4], BF16, "z", z_tag)
+            z_words = z[:].rearrange("p j i -> p (j i)").bitcast(F32).rearrange("p (j u) -> p j u", u=2)
+            for pair in range(width // QUARTER):
+                back = bank(5 + pair % 2, "z_back")
+                for side in range(2):
+                    c0 = QUARTER * pair + P * side
+                    turned = bank(3 + side, "z_sum")
+                    for i in range(4):
+                        nc.tensor.matmul(turned[:, P * i:P * (i + 1)], lhsT=heat_sb[b][:, i, j0 + c0:j0 + c0 + P], rhs=ident[:],
+                                         is_transpose=True, start=(i == 0), stop=False)
+                    for i in range(4):
+                        nc.tensor.matmul(turned[:, P * i:P * (i + 1)], lhsT=x[:, i, c0:c0 + P], rhs=ident[:],
+                                         is_transpose=True, start=False, stop=(i == 3))
+                    z_turned = new_tile([P, 2, P, 2], BF16, "z_turned", last_tag if c0 + P == width else "z_turned%d" % side)
+                    nc.scalar.copy(out=z_turned[:], in_=turned[:].rearrange("j (u e p) -> j u p e", u=2, e=2))
+                    words = z_turned[:].rearrange("j u p e -> j (u p e)").bitcast(F32)
+                    for u in range(2):
+                        nc.tensor.transpose(back[:, QUARTER * side + P * u:QUARTER * side + P * (u + 1)], words[:, P * u:P * (u + 1)], ident[:])
+                nc.scalar.copy(out=z_words[:, QUARTER * pair:QUARTER * (pair + 1), :].rearrange("p (side j) u -> p side j u", side=2),
+                               in_=back[:].rearrange("p (side u j) -> p side j u", side=2, u=2))
             return z
 
         def quantize_z(b, z, j0, width):
             cols = slice(j0, j0 + width)
             nc.vector.quantize_mx(out=z_w[b][:, cols].bitcast(FP8X4), scales=z_s[b][:, cols], in_=z[:].rearrange("p j i -> p (j i)"))
 
-        def open_scores(number, tiles, j0, width):
-            acc = bank(number, "acc")
+        def open_scores(bank_number, row_tiles, j0, width):
+            acc = bank(bank_number, "acc")
             cols = slice(j0, j0 + width)
             half, g0 = divmod(j0, HALF)
-            for k, n in enumerate(tiles):
-                ncols = slice(P * n, P * (n + 1))
-                nc.tensor.matmul_mx(out=acc[:, width * k:width * (k + 1)], lhsT=w4_w[:, ncols].bitcast(FP8X4), lhsT_scale=w4_s[:, ncols],
-                                    rhs=v_w[:, cols].bitcast(FP8X4), rhs_scale=v_s[half][:, g0:g0 + width], start=(k == 0), stop=False)
-                nc.tensor.matmul_mx(out=acc[:, width * k:width * (k + 1)], lhsT=w3_w[0][:, ncols].bitcast(FP8X4), lhsT_scale=w3_s[:, ncols],
+            for m, row_tile in enumerate(row_tiles):
+                ncols = slice(P * row_tile, P * (row_tile + 1))
+                nc.tensor.matmul_mx(out=acc[:, width * m:width * (m + 1)], lhsT=w4_w[:, ncols].bitcast(FP8X4), lhsT_scale=w4_s[:, ncols],
+                                    rhs=v_w[:, cols].bitcast(FP8X4), rhs_scale=v_s[half][:, g0:g0 + width], start=(m == 0), stop=False)
+                nc.tensor.matmul_mx(out=acc[:, width * m:width * (m + 1)], lhsT=w3_w[0][:, ncols].bitcast(FP8X4), lhsT_scale=w3_s[:, ncols],
                                     rhs=z_w[0][:, cols].bitcast(FP8X4), rhs_scale=z_s[0][:, cols], start=False, stop=False)
             return acc
 
-        def close_scores(acc, tiles, j0, width, engine, tag):
+        def close_scores(acc, row_tiles, j0, width, copy_out, tag):
             cols = slice(j0, j0 + width)
-            for k, n in enumerate(tiles):
-                nc.tensor.matmul_mx(out=acc[:, width * k:width * (k + 1)], lhsT=w3_w[1][:, P * n:P * (n + 1)].bitcast(FP8X4),
-                                    lhsT_scale=w3_s[:, N + P * n:N + P * (n + 1)],
-                                    rhs=z_w[1][:, cols].bitcast(FP8X4), rhs_scale=z_s[1][:, cols], start=False, stop=(k == len(tiles) - 1))
-            staged = keep.tile([P, len(tiles), width], F32, name="staged", tag=tag, align_bytes=64)
-            src = acc[:, 0:len(tiles) * width].rearrange("p (k j) -> p k j", k=len(tiles))
-            if engine == "v":
-                nc.vector.tensor_copy(out=staged[:], in_=src)
-            else:
-                nc.scalar.copy(out=staged[:], in_=src)
-            nc.sync.dma_start(out=out[P * tiles[0]:P * (tiles[-1] + 1), cols].rearrange("(k p) j -> p k j", k=len(tiles)), in_=staged[:])
+            count = len(row_tiles)
+            for m, row_tile in enumerate(row_tiles):
+                nc.tensor.matmul_mx(out=acc[:, width * m:width * (m + 1)], lhsT=w3_w[1][:, P * row_tile:P * (row_tile + 1)].bitcast(FP8X4),
+                                    lhsT_scale=w3_s[:, N + P * row_tile:N + P * (row_tile + 1)],
+                                    rhs=z_w[1][:, cols].bitcast(FP8X4), rhs_scale=z_s[1][:, cols], start=False, stop=(m == count - 1))
+            staged = new_tile([P, count, width], F32, "staged", tag)
+            copy_out(out=staged[:], in_=acc[:, 0:count * width].rearrange("p (m j) -> p m j", m=count))
+            nc.sync.dma_start(out=out[P * row_tiles[0]:P * (row_tiles[-1] + 1), cols].rearrange("(m p) j -> p m j", m=count), in_=staged[:])
 
         pick_words(0)
         pick_scales(0, "v_s0")
         pick_words(1)
-        quantize_w1_first(0, "grouped_first")
-        pick_scales(1, "grouped_first")
-        w3_raw1 = keep.tile([P, 4, N], F32, name="w3_raw1", tag="table", align_bytes=64)
+        quantize_w1_first_pass(0, ((0, P // 2), (P // 2, P)), "v_s1")
+        deal_w2_scales(0)
+        pick_scales(1, "v_s1")
+        w3_raw1 = new_tile([P, 4, N], F32, "w3_raw1", "table")
         nc.sync.dma_start(out=w3_raw1[:], in_=w3[HALF:H, :].rearrange("(p i) n -> p i n", i=4))
-        quantize_w1_first(1, "page2")
         first_products(0)
-        larger(0)
+        take_maximum(0)
+        quantize_w1_first_pass(1, ((0, P),), "page2")
+        deal_w2_scales(1)
         for i in (2, 3):
-            pages.append(keep.tile([P, T2], F32, name="page%d" % i, tag="page%d" % i, align_bytes=64))
+            pages.append(new_tile([P, T2], F32, "page%d" % i, "page%d" % i))
             nc.gpsimd.memset(pages[i][:], 0.0)
-        gate0 = [keep.tile([P, 4, HALF], F32, name="gate0_%d" % half, tag="gate_%d" % half, align_bytes=64) for half in range(2)]
+        gate0 = [new_tile([P, 4, HALF], F32, "gate0_%d" % half, "gate_%d" % half) for half in range(2)]
 
         place(0)
         turn_wgt()
         turned_gate(0, 0, gate0, h_tag[1], 0)
         first_products(1)
-        plain_gate(0, gate0, nc.gpsimd)
-        larger(1)
+        plain_gate(0, gate0, stage_left(0), nc.gpsimd)
+        take_maximum(1)
 
         place(1)
         turned_gate(0, 1, gate0, h_tag[2], 0)
         first_products(2)
-        plain_gate(1, gate0, nc.gpsimd)
-        w1_grouped = keep.tile([P, 4, P, 4], BF16, name="w1_grouped", tag="w3_grouped", align_bytes=64)
+        plain_gate(1, gate0, stage_left(1), nc.gpsimd)
+        w1_grouped = new_tile([P, 4, P, 4], BF16, "w1_grouped", "grouped")
         for u in range(2):
-            round_w1(1, u, w1_grouped[:, 2 * u:2 * u + 2])
-        larger(2)
-        w1_w[1] = keep.tile([P, HALF], U32, name="w1_w1", tag="w1_w1", align_bytes=64)
+            round_w1(1, u, w1_grouped[:, 2 * u:2 * u + 2], 0, P)
+        take_maximum(2)
+        w1_w[1] = new_tile([P, HALF], U32, "w1_w1", "w1_w1")
         nc.vector.quantize_mx(out=w1_w[1][:].bitcast(FP8X4), scales=w1_s[:, HALF:S], in_=w1_grouped[:].rearrange("p i q t -> p (i q t)"))
 
         place(2)
         turned_gate(0, 2, gate0, h_tag[3], 0)
         first_products(3)
-        plain_gate(2, gate0, nc.gpsimd)
-        w3_grouped = keep.tile([P, N, 4], BF16, name="w3_grouped0", tag="w3_grouped", align_bytes=64)
-        round_w3(w3_raw0, w3_grouped, 0)
+        plain_gate(2, gate0, stage_left(2), nc.gpsimd)
+        w3_grouped0 = new_tile([P, N, 4], BF16, "w3_grouped0", "grouped")
+        round_w3(w3_raw0, w3_grouped0, 0)
         scale_heat(0, 1)
-        late = keep.tile([P, 4, S], F32, name="gate1", tag="gate_late", align_bytes=64)
-        gate1 = [late[:, :, HALF * half:HALF * (half + 1)] for half in range(2)]
-        turned_gate(1, 0, gate1, "opened", 7)
-        larger(3)
+        gate1_whole = new_tile([P, 4, S], F32, "gate1", "gate_late")
+        gate1 = [gate1_whole[:, :, HALF * half:HALF * (half + 1)] for half in range(2)]
+        turned_gate(1, 0, gate1, "gate_turned", 7)
+        take_maximum(3)
 
         place(3)
         turned_gate(0, 3, gate0, h_tag[4], 0)
         first_products(4)
-        plain_gate(3, gate0, nc.gpsimd)
-        round_w3(w3_raw0, w3_grouped, 1)
+        plain_gate(3, gate0, stage_left(3), nc.gpsimd)
+        round_w3(w3_raw0, w3_grouped0, 1)
         scale_heat(1, 1)
-        turned_gate(1, 1, gate1, "opened", 7)
-        larger(4)
+        turned_gate(1, 1, gate1, "gate_turned", 7)
+        take_maximum(4)
 
-        x = [keep.tile([P, 4, HALF], F32, name="x0_%d" % half, tag=tag, align_bytes=64)[:] for half, tag in enumerate(("h_odd", "x0_late"))]
-        read_pages(x[0], gate0, 0, HALF)
-        read_pages(x[1], gate0, HALF, HALF)
+        x0 = [new_tile([P, 4, HALF], F32, "x0_%d" % half, tag)[:] for half, tag in enumerate(("h_odd", "x_late"))]
+        for half in range(2):
+            read_pages(x0[half], gate0, HALF * half, HALF)
         first_products(5)
-        for i in range(4):
-            scale_heat(i, 0)
-        scale_heat(2, 1)
-        scale_heat(3, 1)
-        round_w3(w3_raw0, w3_grouped, 2)
+        for s in range(4):
+            scale_heat(s, 0)
+        for s in (2, 3):
+            scale_heat(s, 1)
+        round_w3(w3_raw0, w3_grouped0, 2)
 
         place(4)
-        plain_gate(4, gate1, nc.gpsimd)
-        z0 = [finish_z(0, x[0], 0, HALF, "pe", "z_a", h_tag[5])]
-        larger(5)
-        quantize_w3(w3_grouped, 0, "w3_w0")
+        plain_gate(4, gate1, new_tile([P, HALF], F32, "sigmoid4", "gate_1")[:], nc.gpsimd)
+        z0 = [add_heat_by_transposes(0, x0[0], 0, HALF, "z_a", h_tag[5])]
+        take_maximum(5)
+        quantize_w3(w3_grouped0, 0, "w3_w0")
 
         place(5)
         first_products(6)
-        plain_gate(5, gate1, nc.gpsimd)
-        w3_grouped = keep.tile([P, N, 4], BF16, name="w3_grouped1", tag="w3_grouped", align_bytes=64)
-        z0.append(finish_z(0, x[1], HALF, HALF, "pe", "z_b", h_tag[6]))
-        round_w3(w3_raw1, w3_grouped, 0)
-        larger(6)
+        plain_gate(5, gate1, stage_left(5), nc.gpsimd)
+        w3_grouped1 = new_tile([P, N, 4], BF16, "w3_grouped1", "grouped")
+        z0.append(add_heat_by_transposes(0, x0[1], HALF, HALF, "z_b", h_tag[6]))
+        round_w3(w3_raw1, w3_grouped1, 0)
+        take_maximum(6)
 
         place(6)
         turned_gate(1, 2, gate1, h_tag[7], 0)
         first_products(7)
-        plain_gate(6, gate1, nc.gpsimd)
-        round_w3(w3_raw1, w3_grouped, 1)
-        round_w3(w3_raw1, w3_grouped, 2)
-        larger(7)
-        z_w[0] = keep.tile([P, S], U32, name="z_w0", tag="z_w0", align_bytes=64)
+        plain_gate(6, gate1, stage_left(6), nc.gpsimd)
+        for third in (1, 2):
+            round_w3(w3_raw1, w3_grouped1, third)
+        take_maximum(7)
+        z_w[0] = new_tile([P, S], U32, "z_w0", "z_w0")
         for half in range(2):
             quantize_z(0, z0[half], HALF * half, HALF)
-        quantize_w3(w3_grouped, 1, "z_a")
+        quantize_w3(w3_grouped1, 1, "z_a")
 
         place(7)
-        plain_gate(7, gate1, nc.vector)
-        turned_gate(1, 3, gate1, "opened", 3)
+        plain_gate(7, gate1, stage_left(7), nc.vector)
+        turned_gate(1, 3, gate1, "gate_turned", 3)
         for half in range(2):
-            for i in range(4):
-                scale_heat(4 + i, half)
+            for s in range(4, 8):
+                scale_heat(s, half)
 
-        x1 = keep.tile([P, 2, 4, 256], F32, name="x1", tag="h_last", align_bytes=64)
-        starts = [sum(c[0] for c in TAIL[:k]) for k in range(len(TAIL))]
-        groups = [[list(range(6))[g * 6 // len(c[2]):(g + 1) * 6 // len(c[2])] for g in range(len(c[2]))] for c in TAIL]
-        opened = {}
-        stored = []
-        free_slots = ["gate_0", "h_odd", "x0_late", "table", "w3_grouped", "h_even", "tab_s", "gate_1", "opened", "biased", "w2_raw", "st0", "st1"]
-        busy = set()
+        chunks = [(sum(CHUNK_WIDTHS[:c]), width) for c, width in enumerate(CHUNK_WIDTHS)]
+        groups = []
+        for c, (j0, width) in enumerate(chunks):
+            banks_needed = -(-ROW_TILES * width // HALF)
+            per_bank = ROW_TILES // banks_needed
+            groups.extend((c, list(range(first, first + per_bank))) for first in range(0, ROW_TILES, per_bank))
+        free_banks = [0, 1, 2, 6, 7]
+        accs = []
+        acc_banks = []
 
-        def open_what_fits(k):
-            for c in range(len(TAIL)):
-                for g, number in enumerate(TAIL[c][2]):
-                    turning = number in (3, 4, 5) and any(later[1] == "pe" for later in TAIL[k:])
-                    if (c, g) not in opened and number not in busy and not turning:
-                        opened[c, g] = open_scores(number, groups[c][g], starts[c], TAIL[c][0])
-                        busy.add(number)
+        def open_what_fits():
+            for c, row_tiles in groups[len(accs):len(accs) + len(free_banks)]:
+                acc_banks.append(free_banks[0])
+                free_banks.remove(acc_banks[-1])
+                accs.append(open_scores(acc_banks[-1], row_tiles, *chunks[c]))
 
-        open_what_fits(0)
-        for c, (width, road, numbers, engines) in enumerate(TAIL):
-            x = x1[:, c] if c < 2 else keep.tile([P, 4, width], F32, name="x_tail", tag="z_b", align_bytes=64)[:]
-            read_pages(x, gate1, starts[c], width)
-            quantize_z(1, finish_z(1, x, starts[c], width, road, ["z_b", "z_turned1", "z_c0", "z_c1", "z_c0"][c]), starts[c], width)
-            open_what_fits(c + 1)
-            for g, number in enumerate(numbers):
-                close_scores(opened[c, g], groups[c][g], starts[c], width, engines[g], free_slots[len(stored)])
-                stored.append(number)
-                busy.remove(number)
-            open_what_fits(c + 1)
+        staging_tags = ["gate_0", "h_odd", "x_late", "table", "grouped", "h_even", "tab_s", "gate_1", "gate_turned", "biased", "w2_raw",
+                        "staged_a", "staged_b"]
+        x_first = new_tile([P, 2, 4, QUARTER], F32, "x_first", "h_last")
+        x_tags = {2: "z_b", 3: "z_turned1", 4: "z_b"}
+        z_tags = ["z_b", "z_turned1", "z_c", "z_d", "z_c"]
+
+        open_what_fits()
+        for c, (j0, width) in enumerate(chunks):
+            x = x_first[:, c] if c < 2 else new_tile([P, 4, width], F32, "x_tail", x_tags[c])[:]
+            read_pages(x, gate1, j0, width)
+            if c == 0:
+                quantize_z(1, add_heat_by_transposes(1, x, j0, width, z_tags[c], "z_turned1"), j0, width)
+                free_banks.extend((3, 4, 5))
+                open_what_fits()
+            else:
+                quantize_z(1, add_heat_on_vector(1, x, j0, width, z_tags[c]), j0, width)
+            for a in range(len(groups)):
+                if groups[a][0] != c:
+                    continue
+                copy_out = nc.vector.tensor_copy if a == len(groups) - 1 else nc.scalar.copy
+                close_scores(accs[a], groups[a][1], j0, width, copy_out, staging_tags[a])
+                free_banks.append(acc_banks[a])
+            open_what_fits()

from contextlib import ExitStack

import concourse.mybir as mybir
from concourse.masks import make_identity

K, T, S, T2, H, N = 512, 4096, 1024, 2048, 1024, 768
FLOPS = 2 * (2 * K * H * S) + 2 * H * N * S + 2 * K * N * S

F32 = mybir.dt.float32
BF16 = mybir.dt.bfloat16
I32 = mybir.dt.int32
U32 = mybir.dt.uint32
U16 = mybir.dt.uint16
U8 = mybir.dt.uint8
FP8X4 = mybir.dt.float8_e4m3fn_x4
FP4X4 = mybir.dt.float4_e2m1fn_x4
ALU = mybir.AluOpType
ACT = mybir.ActivationFunctionType

P = 128
HALF = 512
QUARTER = 256
ROW_TILES = N // P
DRIFT = 8
CHUNK_WIDTHS = [QUARTER, QUARTER, QUARTER, P, P]


def tile_list_roast_phase_scores_kernel(tc, tab_words, tab_scales, offs, w1, b1, w2_words, w2_scales, wgs, offs2, wgt,
                                                  offs3, heat, hg, w3, w4_words, w4_scales, out):
    nc = tc.nc
    with ExitStack() as ctx:
        sbuf = ctx.enter_context(tc.tile_pool(name="sbuf", bufs=1))
        psum = ctx.enter_context(tc.psum_pool(name="psum", bufs=1))

        def new_tile(shape, dtype, name, tag):
            return sbuf.tile(shape, dtype, name=name, tag=tag, align_bytes=64)

        def bank(number, name):
            return psum.tile([P, HALF], F32, tag="bank%d" % number, name=name)

        def load_scale_rows(scales, rows):
            for quad in range(4):
                nc.sync.dma_start(out=scales[32 * quad:32 * quad + 4, :].bitcast(I32), in_=rows[4 * quad:4 * quad + 4, :].bitcast(I32))

        list1 = sbuf.tile([P, S // 16], U16, name="list1")
        list2 = sbuf.tile([P, S // 16], U16, name="list2")
        list3 = sbuf.tile([P, S // 16], U16, name="list3")
        tab_s = new_tile([P, T], U8, "tab_s", "tab_s")
        w2_s_raw = new_tile([P, H], U8, "w2_s_raw", "w2_s_raw")
        w4_s = new_tile([P, N], U8, "w4_s", "w4_s")
        nc.gpsimd.memset(w2_s_raw[:].bitcast(I32), 0)
        nc.vector.memset(tab_s[:].bitcast(I32), 0)
        nc.vector.memset(w4_s[:].bitcast(I32), 0)

        w2_raw = new_tile([P, 2 * H], U8, "w2_raw", "w2_raw")
        nc.sync.dma_start(out=w2_raw[:].bitcast(I32), in_=w2_words[0].bitcast(I32))
        tab_w = new_tile([P, T], I32, "tab_w", "table")
        nc.sync.dma_start(out=tab_w[:], in_=tab_words[0].rearrange("p t i -> p (t i)").bitcast(I32))
        nc.sync.dma_start(list1[:], offs)
        load_scale_rows(tab_s, tab_scales[0])

        w1_raw = [new_tile([P, 4, HALF], F32, "w1_raw0", "gate_0"), new_tile([P, 4, HALF], F32, "w1_raw1", "gate_late")]
        for c0 in (0, QUARTER):
            nc.sync.dma_start(out=w1_raw[0][:, :, c0:c0 + QUARTER], in_=w1[:, c0:c0 + QUARTER].rearrange("(p t) c -> p t c", t=4))
        b1_sb = sbuf.tile([P, 2, 4], F32, name="b1_sb")
        nc.sync.dma_start(out=b1_sb[:], in_=b1.rearrange("(b p i) -> p b i", b=2, i=4))
        load_scale_rows(w2_s_raw, w2_scales[0])
        wgs_sb = sbuf.tile([P, S], F32, name="wgs_sb")
        nc.sync.dma_start(out=wgs_sb[:], in_=wgs)
        nc.sync.dma_start(list2[:], offs2)
        heat_sb = [sbuf.tile([P, 4, S], F32, name="heat%d" % b) for b in range(2)]
        wgt_sb = sbuf.tile([P, S], F32, name="wgt_sb")
        nc.sync.dma_start(out=wgt_sb[:], in_=wgt)
        for i0 in (0, 2):
            nc.sync.dma_start(out=heat_sb[0][:, i0:i0 + 2, :], in_=heat[0:HALF, :].rearrange("(p i) j -> p i j", i=4)[:, i0:i0 + 2, :])
        hg_sb = sbuf.tile([P, 2, 4], F32, name="hg_sb")
        nc.sync.dma_start(out=hg_sb[:], in_=hg.rearrange("(b p i) -> p b i", b=2, i=4))
        nc.sync.dma_start(list3[:], offs3)
        nc.sync.dma_start(out=w1_raw[1][:], in_=w1[:, HALF:H].rearrange("(p t) c -> p t c", t=4))
        nc.sync.dma_start(out=heat_sb[1][:], in_=heat[HALF:H, :].rearrange("(p i) j -> p i j", i=4))
        w4_w = new_tile([P, N], I32, "w4_w", "w4_w")
        nc.sync.dma_start(out=w4_w[:], in_=w4_words[0].rearrange("p c i -> p (c i)").bitcast(I32))
        load_scale_rows(w4_s, w4_scales[0])
        w3_raw0 = new_tile([P, 4, N], F32, "w3_raw0", "h_last")
        nc.sync.dma_start(out=w3_raw0[:], in_=w3[0:HALF, :].rearrange("(p i) n -> p i n", i=4))

        ident = sbuf.tile([P, P], F32, name="ident")
        make_identity(nc, ident[:])

        pages = [sbuf.tile([P, T2], F32, name="page%d" % i) for i in range(2)]
        for page in pages:
            nc.vector.memset(page[:], 0.0)

        w2_w = new_tile([P, 2, 4, P, 2], U8, "w2_w", "w2_w")
        w2_s = new_tile([P, 2, 4, P], U8, "w2_s", "w2_s")
        for b in range(2):
            nc.vector.tensor_copy(out=w2_w[:, b], in_=w2_raw[:, 2 * HALF * b:2 * HALF * (b + 1)].rearrange("p (q i e) -> p i q e", i=4, e=2))

        def deal_w2_scales(b):
            nc.vector.tensor_copy(out=w2_s[:, b], in_=w2_s_raw[:, HALF * b:HALF * (b + 1)].rearrange("p (q i) -> p i q", i=4))

        v_w = new_tile([P, S], U32, "v_w", "v_w")
        v_s = {}

        def pick_words(half):
            nc.vector.tensor_copy(v_w[:, HALF * half:HALF * (half + 1)], tab_w[:].bitcast(U32).indirect(list1[:, 32 * half:32 * (half + 1)]))

        def pick_scales(half, tag):
            v_s[half] = new_tile([P, HALF], U8, "v_s%d" % half, tag)
            nc.vector.tensor_copy(v_s[half][:], tab_s[:].indirect(list1[:, 32 * half:32 * (half + 1)]))

        w1_w = {0: new_tile([P, HALF], U32, "w1_w0", "w1_w0")}
        w1_s = new_tile([P, 8 * P], U8, "w1_s", "w1_s")

        def round_w1(b, u, grouped, q0, q1):
            nc.scalar.copy(out=grouped.rearrange("p e q t -> p q t e")[:, q0:q1],
                           in_=w1_raw[b][:].rearrange("p t (q i) -> p q t i", i=4)[:, q0:q1, :, 2 * u:2 * u + 2])

        def quantize_w1_first_pass(u, q_ranges, tag):
            grouped = new_tile([P, 2, P, 4], BF16, "w1_grouped", tag)
            for q0, q1 in q_ranges:
                round_w1(0, u, grouped[:], q0, q1)
            cols = slice(2 * P * u, 2 * P * (u + 1))
            nc.vector.quantize_mx(out=w1_w[0][:, cols].bitcast(FP8X4), scales=w1_s[:, cols], in_=grouped[:].rearrange("p e q t -> p (e q t)"))

        w3_w = {}
        w3_s = new_tile([P, 2 * N], U8, "w3_s", "w3_s")

        def round_w3(raw, grouped, third):
            cols = slice(QUARTER * third, QUARTER * (third + 1))
            nc.scalar.copy(out=grouped[:, cols, :].rearrange("p (c e) t -> p c t e", e=4), in_=raw[:, :, cols].rearrange("p t (c e) -> p c t e", e=4))

        def quantize_w3(grouped, b, tag):
            w3_w[b] = new_tile([P, N], U32, "w3_w%d" % b, tag)
            for c0, c1 in ((0, HALF), (HALF, N)):
                nc.vector.quantize_mx(out=w3_w[b][:, c0:c1].bitcast(FP8X4), scales=w3_s[:, N * b + c0:N * b + c1],
                                      in_=grouped[:, c0:c1, :].rearrange("p n t -> p (n t)"))

        h_tag = ["h_even", "h_odd", "h_even", "h_odd", "h_even", "tab_s", "h_even", "h_last"]
        follows_maximum = {0: "page3", 2: "w1_w1", 4: "x_late", 5: "w3_w0", 7: "z_w0"}
        stage = sbuf.tile([P, S + 8 * DRIFT], F32, name="stage")
        products = {}
        h_tiles = {}

        def first_products(s):
            b, i = divmod(s, 4)
            for half in ((0, 1) if s == 0 else (1, 0)):
                cols = slice(HALF * half, HALF * (half + 1))
                if half == 0:
                    biased = new_tile([P, HALF], F32, "biased", follows_maximum.get(s, "biased"))[:]
                else:
                    biased = stage[:, HALF + DRIFT * s:S + DRIFT * s]
                read1 = bank(7 if s < 2 and half == 1 else 2, "read1")
                nc.tensor.matmul_mx(out=read1[:], lhsT=w1_w[b][:, P * i:P * (i + 1)].bitcast(FP8X4), lhsT_scale=w1_s[:, P * s:P * (s + 1)],
                                    rhs=v_w[:, cols].bitcast(FP8X4), rhs_scale=v_s[half][:], start=True, stop=True)
                read2 = bank(half, "read2")
                nc.tensor.matmul_mx(out=read2[:], lhsT=w2_w[:, b, i].rearrange("p q e -> p (q e)").bitcast(FP4X4), lhsT_scale=w2_s[:, b, i],
                                    rhs=v_w[:, cols].bitcast(FP8X4), rhs_scale=v_s[half][:], start=True, stop=True)
                nc.scalar.activation(biased, read1[:], ACT.Identity, bias=b1_sb[:, b, i:i + 1])
                products[s, half] = (read2, biased)

        def take_maximum(s):
            h_tiles[s] = new_tile([P, S], F32, "h%d" % s, h_tag[s])
            for half in range(2):
                read2, biased = products[s, half]
                nc.vector.tensor_tensor(h_tiles[s][:, HALF * half:HALF * (half + 1)], read2[:], biased, ALU.max)

        def place(s):
            nc.vector.tensor_tensor(pages[s % 4][:].indirect(list2[:]), h_tiles[s][:], wgs_sb[:], ALU.mult)

        wgt_turned = sbuf.tile([P, 4, 8], F32, name="wgt_turned")

        def turn_wgt():
            turned = bank(3, "wgt_bank")
            for blk in range(4):
                nc.tensor.transpose(turned[:, P * blk:P * (blk + 1)], wgt_sb[:, P * blk:P * (blk + 1)], ident[:])
            nc.scalar.copy(out=wgt_turned[:], in_=turned[:].rearrange("j (blk g q) -> j blk g q", blk=4, g=8)[:, :, :, 0])

        def turned_gate(b, blk, gate, tag, bank_number):
            cols = slice(P * blk, P * (blk + 1))
            turned = bank(bank_number, "heat_turned")
            for i in range(4):
                nc.tensor.transpose(turned[:, P * i:P * (i + 1)], heat_sb[b][:, i, cols], ident[:])
            gate_turned = new_tile([P, 4, P], F32, "gate_turned", tag)
            nc.scalar.activation(gate_turned[:].rearrange("j i p -> j (i p)"), turned[:], ACT.Sigmoid)
            for g in range(8):
                group = gate_turned[:, :, 16 * g:16 * (g + 1)]
                nc.scalar.activation(group, group, ACT.Copy, scale=wgt_turned[:, blk, g:g + 1])
            back = bank(5 + blk % 2, "gate_back")
            for i in range(4):
                nc.tensor.transpose(back[:, P * i:P * (i + 1)], gate_turned[:, i, :], ident[:])
            nc.scalar.copy(out=gate[0][:, :, cols], in_=back[:].rearrange("p (i j) -> p i j", i=4))

        def plain_gate(s, gate, sigmoid, engine):
            b, i = divmod(s, 4)
            nc.scalar.activation(sigmoid, heat_sb[b][:, i, HALF:S], ACT.Sigmoid)
            engine.tensor_tensor(gate[1][:, i, :], sigmoid, wgt_sb[:, HALF:S], ALU.mult)

        def stage_left(s):
            return stage[:, DRIFT * (s + 1):HALF + DRIFT * (s + 1)]

        def scale_heat(s, half):
            b, i = divmod(s, 4)
            part = heat_sb[b][:, i, HALF * half:HALF * (half + 1)]
            nc.scalar.activation(part, part, ACT.Copy, scale=hg_sb[:, b, i:i + 1])

        z_w = {1: new_tile([P, S], U32, "z_w1", "z_w1")}
        z_s = [new_tile([P, S], U8, "z_s%d" % b, "z_s%d" % b) for b in range(2)]

        def read_pages(x, gate, j0, width):
            half, g0 = divmod(j0, HALF)
            for i in range(4):
                nc.vector.tensor_tensor(x[:, i, :], pages[i][:].indirect(list3[:, j0 // 16:(j0 + width) // 16]),
                                        gate[half][:, i, g0:g0 + width], ALU.mult)

        def add_heat_on_vector(b, x, j0, width, z_tag):
            z = new_tile([P, width, 4], BF16, "z", z_tag)
            nc.vector.tensor_tensor(z[:].rearrange("p (c e) i -> p c i e", e=4), x.rearrange("p i (c e) -> p c i e", e=4),
                                    heat_sb[b][:, :, j0:j0 + width].rearrange("p i (c e) -> p c i e", e=4), ALU.add)
            return z

        def add_heat_by_transposes(b, x, j0, width, z_tag, last_tag):
            z = new_tile([P, width, 4], BF16, "z", z_tag)
            z_words = z[:].rearrange("p j i -> p (j i)").bitcast(F32).rearrange("p (j u) -> p j u", u=2)
            for pair in range(width // QUARTER):
                back = bank(5 + pair % 2, "z_back")
                for side in range(2):
                    c0 = QUARTER * pair + P * side
                    turned = bank(3 + side, "z_sum")
                    for i in range(4):
                        nc.tensor.matmul(turned[:, P * i:P * (i + 1)], lhsT=heat_sb[b][:, i, j0 + c0:j0 + c0 + P], rhs=ident[:],
                                         is_transpose=True, start=(i == 0), stop=False)
                    for i in range(4):
                        nc.tensor.matmul(turned[:, P * i:P * (i + 1)], lhsT=x[:, i, c0:c0 + P], rhs=ident[:],
                                         is_transpose=True, start=False, stop=(i == 3))
                    z_turned = new_tile([P, 2, P, 2], BF16, "z_turned", last_tag if c0 + P == width else "z_turned%d" % side)
                    nc.scalar.copy(out=z_turned[:], in_=turned[:].rearrange("j (u e p) -> j u p e", u=2, e=2))
                    words = z_turned[:].rearrange("j u p e -> j (u p e)").bitcast(F32)
                    for u in range(2):
                        nc.tensor.transpose(back[:, QUARTER * side + P * u:QUARTER * side + P * (u + 1)], words[:, P * u:P * (u + 1)], ident[:])
                nc.scalar.copy(out=z_words[:, QUARTER * pair:QUARTER * (pair + 1), :].rearrange("p (side j) u -> p side j u", side=2),
                               in_=back[:].rearrange("p (side u j) -> p side j u", side=2, u=2))
            return z

        def quantize_z(b, z, j0, width):
            cols = slice(j0, j0 + width)
            nc.vector.quantize_mx(out=z_w[b][:, cols].bitcast(FP8X4), scales=z_s[b][:, cols], in_=z[:].rearrange("p j i -> p (j i)"))

        def open_scores(bank_number, row_tiles, j0, width):
            acc = bank(bank_number, "acc")
            cols = slice(j0, j0 + width)
            half, g0 = divmod(j0, HALF)
            for m, row_tile in enumerate(row_tiles):
                ncols = slice(P * row_tile, P * (row_tile + 1))
                nc.tensor.matmul_mx(out=acc[:, width * m:width * (m + 1)], lhsT=w4_w[:, ncols].bitcast(FP8X4), lhsT_scale=w4_s[:, ncols],
                                    rhs=v_w[:, cols].bitcast(FP8X4), rhs_scale=v_s[half][:, g0:g0 + width], start=(m == 0), stop=False)
                nc.tensor.matmul_mx(out=acc[:, width * m:width * (m + 1)], lhsT=w3_w[0][:, ncols].bitcast(FP8X4), lhsT_scale=w3_s[:, ncols],
                                    rhs=z_w[0][:, cols].bitcast(FP8X4), rhs_scale=z_s[0][:, cols], start=False, stop=False)
            return acc

        def close_scores(acc, row_tiles, j0, width, copy_out, tag):
            cols = slice(j0, j0 + width)
            count = len(row_tiles)
            for m, row_tile in enumerate(row_tiles):
                nc.tensor.matmul_mx(out=acc[:, width * m:width * (m + 1)], lhsT=w3_w[1][:, P * row_tile:P * (row_tile + 1)].bitcast(FP8X4),
                                    lhsT_scale=w3_s[:, N + P * row_tile:N + P * (row_tile + 1)],
                                    rhs=z_w[1][:, cols].bitcast(FP8X4), rhs_scale=z_s[1][:, cols], start=False, stop=(m == count - 1))
            staged = new_tile([P, count, width], F32, "staged", tag)
            copy_out(out=staged[:], in_=acc[:, 0:count * width].rearrange("p (m j) -> p m j", m=count))
            nc.sync.dma_start(out=out[P * row_tiles[0]:P * (row_tiles[-1] + 1), cols].rearrange("(m p) j -> p m j", m=count), in_=staged[:])

        pick_words(0)
        pick_scales(0, "v_s0")
        pick_words(1)
        quantize_w1_first_pass(0, ((0, P // 2), (P // 2, P)), "v_s1")
        deal_w2_scales(0)
        pick_scales(1, "v_s1")
        w3_raw1 = new_tile([P, 4, N], F32, "w3_raw1", "table")
        nc.sync.dma_start(out=w3_raw1[:], in_=w3[HALF:H, :].rearrange("(p i) n -> p i n", i=4))
        first_products(0)
        take_maximum(0)
        quantize_w1_first_pass(1, ((0, P),), "page2")
        deal_w2_scales(1)
        for i in (2, 3):
            pages.append(new_tile([P, T2], F32, "page%d" % i, "page%d" % i))
            nc.gpsimd.memset(pages[i][:], 0.0)
        gate0 = [new_tile([P, 4, HALF], F32, "gate0_%d" % half, "gate_%d" % half) for half in range(2)]

        place(0)
        turn_wgt()
        turned_gate(0, 0, gate0, h_tag[1], 0)
        first_products(1)
        plain_gate(0, gate0, stage_left(0), nc.gpsimd)
        take_maximum(1)

        place(1)
        turned_gate(0, 1, gate0, h_tag[2], 0)
        first_products(2)
        plain_gate(1, gate0, stage_left(1), nc.gpsimd)
        w1_grouped = new_tile([P, 4, P, 4], BF16, "w1_grouped", "grouped")
        for u in range(2):
            round_w1(1, u, w1_grouped[:, 2 * u:2 * u + 2], 0, P)
        take_maximum(2)
        w1_w[1] = new_tile([P, HALF], U32, "w1_w1", "w1_w1")
        nc.vector.quantize_mx(out=w1_w[1][:].bitcast(FP8X4), scales=w1_s[:, HALF:S], in_=w1_grouped[:].rearrange("p i q t -> p (i q t)"))

        place(2)
        turned_gate(0, 2, gate0, h_tag[3], 0)
        first_products(3)
        plain_gate(2, gate0, stage_left(2), nc.gpsimd)
        w3_grouped0 = new_tile([P, N, 4], BF16, "w3_grouped0", "grouped")
        round_w3(w3_raw0, w3_grouped0, 0)
        scale_heat(0, 1)
        gate1_whole = new_tile([P, 4, S], F32, "gate1", "gate_late")
        gate1 = [gate1_whole[:, :, HALF * half:HALF * (half + 1)] for half in range(2)]
        turned_gate(1, 0, gate1, "gate_turned", 7)
        take_maximum(3)

        place(3)
        turned_gate(0, 3, gate0, h_tag[4], 0)
        first_products(4)
        plain_gate(3, gate0, stage_left(3), nc.gpsimd)
        round_w3(w3_raw0, w3_grouped0, 1)
        scale_heat(1, 1)
        turned_gate(1, 1, gate1, "gate_turned", 7)
        take_maximum(4)

        x0 = [new_tile([P, 4, HALF], F32, "x0_%d" % half, tag)[:] for half, tag in enumerate(("h_odd", "x_late"))]
        for half in range(2):
            read_pages(x0[half], gate0, HALF * half, HALF)
        first_products(5)
        for s in range(4):
            scale_heat(s, 0)
        for s in (2, 3):
            scale_heat(s, 1)
        round_w3(w3_raw0, w3_grouped0, 2)

        place(4)
        plain_gate(4, gate1, new_tile([P, HALF], F32, "sigmoid4", "gate_1")[:], nc.gpsimd)
        z0 = [add_heat_by_transposes(0, x0[0], 0, HALF, "z_a", h_tag[5])]
        take_maximum(5)
        quantize_w3(w3_grouped0, 0, "w3_w0")

        place(5)
        first_products(6)
        plain_gate(5, gate1, stage_left(5), nc.gpsimd)
        w3_grouped1 = new_tile([P, N, 4], BF16, "w3_grouped1", "grouped")
        z0.append(add_heat_by_transposes(0, x0[1], HALF, HALF, "z_b", h_tag[6]))
        round_w3(w3_raw1, w3_grouped1, 0)
        take_maximum(6)

        place(6)
        turned_gate(1, 2, gate1, h_tag[7], 0)
        first_products(7)
        plain_gate(6, gate1, stage_left(6), nc.gpsimd)
        for third in (1, 2):
            round_w3(w3_raw1, w3_grouped1, third)
        take_maximum(7)
        z_w[0] = new_tile([P, S], U32, "z_w0", "z_w0")
        for half in range(2):
            quantize_z(0, z0[half], HALF * half, HALF)
        quantize_w3(w3_grouped1, 1, "z_a")

        place(7)
        plain_gate(7, gate1, stage_left(7), nc.vector)
        turned_gate(1, 3, gate1, "gate_turned", 3)
        for half in range(2):
            for s in range(4, 8):
                scale_heat(s, half)

        chunks = [(sum(CHUNK_WIDTHS[:c]), width) for c, width in enumerate(CHUNK_WIDTHS)]
        groups = []
        for c, (j0, width) in enumerate(chunks):
            banks_needed = -(-ROW_TILES * width // HALF)
            per_bank = ROW_TILES // banks_needed
            groups.extend((c, list(range(first, first + per_bank))) for first in range(0, ROW_TILES, per_bank))
        free_banks = [0, 1, 2, 6, 7]
        accs = []
        acc_banks = []

        def open_what_fits():
            for c, row_tiles in groups[len(accs):len(accs) + len(free_banks)]:
                acc_banks.append(free_banks[0])
                free_banks.remove(acc_banks[-1])
                accs.append(open_scores(acc_banks[-1], row_tiles, *chunks[c]))

        staging_tags = ["gate_0", "h_odd", "x_late", "table", "grouped", "h_even", "tab_s", "gate_1", "gate_turned", "biased", "w2_raw",
                        "staged_a", "staged_b"]
        x_first = new_tile([P, 2, 4, QUARTER], F32, "x_first", "h_last")
        x_tags = {2: "z_b", 3: "z_turned1", 4: "z_b"}
        z_tags = ["z_b", "z_turned1", "z_c", "z_d", "z_c"]

        open_what_fits()
        for c, (j0, width) in enumerate(chunks):
            x = x_first[:, c] if c < 2 else new_tile([P, 4, width], F32, "x_tail", x_tags[c])[:]
            read_pages(x, gate1, j0, width)
            if c == 0:
                quantize_z(1, add_heat_by_transposes(1, x, j0, width, z_tags[c], "z_turned1"), j0, width)
                free_banks.extend((3, 4, 5))
                open_what_fits()
            else:
                quantize_z(1, add_heat_on_vector(1, x, j0, width, z_tags[c]), j0, width)
            for a in range(len(groups)):
                if groups[a][0] != c:
                    continue
                copy_out = nc.vector.tensor_copy if a == len(groups) - 1 else nc.scalar.copy
                close_scores(accs[a], groups[a][1], j0, width, copy_out, staging_tags[a])
                free_banks.append(acc_banks[a])
            open_what_fits()
